import numpy as np
import ml_dtypes


def mxq(x, axis, fmt="e4m3"):
    dtype, down = {"e4m3": (ml_dtypes.float8_e4m3fn, 7), "e5m2": (ml_dtypes.float8_e5m2, 14)}[fmt]
    v = np.moveaxis(np.asarray(x, np.float32).astype(ml_dtypes.bfloat16).astype(np.float64), axis, -1)
    blocks = v.reshape(v.shape[:-1] + (-1, 32))
    amax = np.abs(blocks).max(-1, keepdims=True)
    byte = np.maximum(np.where(amax > 0, np.frexp(amax)[1] - 1 + 127, 0) - down, 1)
    scale = np.exp2(byte - 127.0)
    codes = (blocks / scale).astype(np.float32).astype(dtype).astype(np.float64)
    return np.moveaxis((codes * scale).reshape(v.shape), -1, axis)


WIDE = False


def mx_kscale(k):
    if not WIDE:
        return np.ones(k)
    levels = np.array([10, -10, 5, -5, 0])
    if k % 512:
        return np.exp2(np.random.permutation(np.resize(levels, k // 32))).repeat(32)
    a = np.empty((k // 512, 16))
    for p in range(k // 512):
        a[p, :8] = np.random.permutation(np.resize(levels, 8))
        for g in range(8):
            far = levels[np.abs(levels - a[p, g]) >= 10]
            a[p, g + 8] = far[np.random.randint(len(far))]
    return np.exp2(a.ravel()).repeat(32)


BF16 = ml_dtypes.bfloat16


def bf(x):
    return np.asarray(x, np.float32).astype(BF16)


def f64(x):
    return np.asarray(x).astype(np.float64)

def planes(Y):
    n, m = Y.shape
    b = f64(bf(Y)).reshape(n // 32, 32, m)
    amax = np.abs(b).max(1)
    byte = np.clip(np.where(amax > 0, np.frexp(amax)[1] - 1 + 127 - 7, 1), 1, 254)
    codes = (b * np.exp2(127.0 - byte)[:, None, :]).reshape(n, m).astype(np.float32).astype(ml_dtypes.float8_e4m3fn).view(np.uint8)
    words = codes.reshape(n // 512, 128, 4, m).transpose(0, 1, 3, 2)
    return np.ascontiguousarray(words), np.ascontiguousarray(byte.astype(np.uint8).reshape(n // 512, 16, m))


T, D, F = 1024, 1024, 2048

SPREAD = 0.8
MEMORY = 0.5

def noise(*shape):
    return np.random.randn(*shape)

def setup_inputs():
    size = np.exp(SPREAD * noise(D))
    sa = mx_kscale(T)
    sb = mx_kscale(T)
    return {
        "xa": bf(noise(T, D) * size[None, :] * sa[:, None]),
        "dza": bf(noise(T, F) / np.sqrt(T) / sa[:, None]),
        "xb": bf(noise(T, D) * size[None, :] * sb[:, None]),
        "dzb": bf(noise(T, F) / np.sqrt(T) / sb[:, None]),
        "clip_a": bf(0.3 + 0.7 * np.random.rand(F)),
        "clip_b": bf(0.3 + 0.7 * np.random.rand(F)),
        "memory": bf(MEMORY * noise(D, F) * size[:, None]),
    }

def reference(xa, dza, xb, dzb, clip_a, clip_b, memory):
    qxa = mxq(f64(xa), 0, "e4m3")
    qza = mxq(f64(dza), 0, "e4m3")
    qxb = mxq(f64(xb), 0, "e4m3")
    qzb = mxq(f64(dzb), 0, "e4m3")
    ga = qxa.T @ qza
    gb = qxb.T @ qzb
    y = ga * f64(clip_a)[None, :] + gb * f64(clip_b)[None, :] + f64(memory)
    Y = y.reshape(D, F)
    words, scales = planes(Y)
    return y, words, scales

@@ -1,0 +1,306 @@
+from contextlib import ExitStack
+
+import concourse.mybir as mybir
+from concourse.masks import make_identity
+
+T, D, F = 1024, 1024, 2048
+FLOPS = 2 * 2 * T * D * F
+
+F32 = mybir.dt.float32
+BF16 = mybir.dt.bfloat16
+U32 = mybir.dt.uint32
+I32 = mybir.dt.int32
+U8 = mybir.dt.uint8
+FP8X4 = mybir.dt.float8_e4m3fn_x4
+ALU = mybir.AluOpType
+ACT = mybir.ActivationFunctionType
+
+P = 128
+PACK = 4
+KP = P * PACK
+W = 512
+H = 256
+
+ORDER = [(0, 0), (1, 0), (0, 1), (1, 1)] + [(j, g) for j in range(2, 8) for g in range(2)]
+VS = [496, 304, 176, 400, 224, 400, 224, 208, 224, 400, 304, 272, 32, 0, 0, 16, 48, 48, 0, 0, 16, 0, 0, 0]
+VP = [10, 12, 11, 14, 15, 16, 14, 18, 19, 20, 21, 22, 23, 24, 24, 23, 24]
+CP = [13, 20, 26, 24, 22, 27, 28, 30, 27, 29, 32, 32, 34, 36, 31, 38, 38, 40, 41, 42, 44, 41, 42, 46, 50, 55, 46, 48, 48, 49, 57, 50]
+LP = [23, 25, 34, 34, 35, 36, 34, 36, 34, 36, 36, 35, 34, 34, 34, 36]
+FENG = "GGGGGGGGGGGGGGSS"
+STAGE_BUFS = 4
+AB_BUFS = 3
+TB_BUFS = 2
+SPLIT0 = 1
+GS = [0, 0, 0, 0, 0, 0, 0, 0, 0, 0, 0, 0, 0, 0, 0, 0, 0, 0, 0, 0, 0, 0, 0, 0]
+QO_FIRST = 0
+ACC = []
+A_BUFS = 3
+MP = [18, 21, 22, 22, 28, 34, 44, 35]
+
+
+def tile_replica_weight_grad_g2_kernel(tc, xa, dza, xb, dzb, clip_a, clip_b, memory, out_0, out_1, out_2):
+    nc = tc.nc
+    xs, dzs = (xa, xb), (dza, dzb)
+    steps = ORDER
+    units, loads = [], []
+    for j, g in steps:
+        for r in range(2):
+            for u in [("x", r, 0, g), ("x", r, 1, g), ("z", r, j)]:
+                if u not in units:
+                    units.append(u)
+                    if u[0] == "x":
+                        loads.append(u)
+                    elif j < 2 * SPLIT0:
+                        loads += [("h", r, 0, j), ("h", r, 1, j)]
+                    elif j % 2 == 0:
+                        loads += [("z", r, 0, j // 2), ("z", r, 1, j // 2)]
+    need = []
+    for j, g in steps:
+        if ("m", g, j // 2) not in need:
+            need.append(("m", g, j // 2))
+    for key, at in zip(need, MP):
+        loads.insert(at, key)
+
+    with ExitStack() as ctx:
+        keep = ctx.enter_context(tc.tile_pool(name="keep", bufs=1))
+        work = ctx.enter_context(tc.tile_pool(name="work", bufs=3))
+        psum = ctx.enter_context(tc.psum_pool(name="psum", bufs=1))
+        ctx.enter_context(tc.manual_schedule())
+
+        raw, stage, codes, scales, banks, first, both, turned, ys, ybf, words = {}, {}, {}, {}, {}, {}, {}, {}, {}, {}, {}
+
+        def load(key):
+            if key[0] == "m":
+                g, q = key[1:]
+                src, tag, bufs = memory[g * KP:(g + 1) * KP, q * W:(q + 1) * W], "mem", 8
+            elif key[0] == "h":
+                r, s, c = key[1:]
+                src, tag, bufs = dzs[r][s * KP:(s + 1) * KP, c * H:(c + 1) * H], "half", 8 * SPLIT0
+            else:
+                r, s, c = key[1:]
+                src, tag, bufs = (xs if key[0] == "x" else dzs)[r][s * KP:(s + 1) * KP, c * W:(c + 1) * W], "raw", 24 - 4 * SPLIT0
+            raw[key] = work.tile([P, PACK, src.shape[1]], BF16, name=tag, tag=tag, bufs=bufs)
+            nc.sync.dma_start(out=raw[key][:], in_=src.rearrange("(p t) c -> p t c", t=PACK))
+
+        def weave(eng, dst, src):
+            dst = dst.rearrange("p (c i) t -> p c t i", i=4)
+            src = src.rearrange("p t (c i) -> p c t i", i=4)
+            if eng == "V":
+                nc.vector.tensor_copy(out=dst, in_=src)
+            elif eng == "S":
+                nc.scalar.copy(out=dst, in_=src)
+            else:
+                nc.gpsimd.tensor_scalar(out=dst, in0=src, scalar1=1.0, scalar2=0.0, op0=ALU.mult, op1=ALU.add)
+
+        def weave_unit(i, eng, lo, hi):
+            u = units[i]
+            if i not in stage:
+                stage[i] = work.tile([P, W, PACK], BF16, name="stage", tag="stage%d" % (i % STAGE_BUFS), bufs=1, align_bytes=64)
+            if u[0] == "x":
+                if hi > lo:
+                    weave(eng, stage[i][:, lo:hi, :], raw[u][:, :, lo:hi])
+                return
+            r, j = u[1:]
+            for s in range(2):
+                a, b = max(lo, s * H), min(hi, (s + 1) * H)
+                if b > a:
+                    if j < 2 * SPLIT0:
+                        src, off = raw["h", r, s, j], -s * H
+                    else:
+                        src, off = raw["z", r, s, j // 2], (j % 2) * H - s * H
+                    weave(eng, stage[i][:, a:b, :], src[:, :, a + off:b + off])
+
+        def quant_in(i):
+            u = units[i]
+            tag, bufs = ("xq", 8) if u[0] == "x" else ("zq", 6)
+            codes[u] = work.tile([P, W], U32, name=tag + "c", tag=tag + "c", bufs=bufs, align_bytes=64)
+            scales[u] = work.tile([P, W], U8, name=tag + "s", tag=tag + "s", bufs=bufs, align_bytes=64)
+            nc.vector.quantize_mx(out=codes[u][:].bitcast(FP8X4), scales=scales[u][:], in_=stage[i][:].rearrange("p c t -> p (c t)"))
+
+        def products(h):
+            j, g = steps[h]
+            for u in range(2):
+                for r in range(2):
+                    banks[h, u, r] = psum.tile([P, W], F32, name="ab"[r], tag="ab"[r], bufs=(A_BUFS, AB_BUFS)[r])
+                    for s in range(2):
+                        cols = slice(s * H + u * P, s * H + (u + 1) * P)
+                        nc.tensor.matmul_mx(
+                            out=banks[h, u, r][:],
+                            lhsT=codes["z", r, j][:, cols].bitcast(FP8X4), lhsT_scale=scales["z", r, j][:, cols],
+                            rhs=codes["x", r, s, g][:].bitcast(FP8X4), rhs_scale=scales["x", r, s, g][:],
+                            start=(s == 0), stop=(s == 1))
+
+        def clip_first(h, u):
+            c = 2 * steps[h][0] + u
+            first[h, u] = work.tile([P, PACK, P], F32, name="first", tag="first", bufs=4)
+            nc.scalar.activation(out=first[h, u][:], in_=banks[h, u, 0][:].rearrange("p (m t) -> p t m", t=PACK),
+                                 func=ACT.Copy, scale=clips[:, c:c + 1])
+
+        def clip_second(h, u):
+            c = 16 + 2 * steps[h][0] + u
+            both[h, u] = work.tile([P, PACK, P], F32, name="both", tag="both", bufs=4)
+            if h in ACC:
+                nc.scalar.activation(out=both[h, u][:], in_=banks[h, u, 1][:].rearrange("p (m t) -> p t m", t=PACK),
+                                     func=ACT.Copy, scale=clips[:, c:c + 1])
+                return
+            nc.vector.scalar_tensor_tensor(out=both[h, u][:], in0=banks[h, u, 1][:].rearrange("p (m t) -> p t m", t=PACK),
+                                           scalar=clips[:, c:c + 1], in1=first[h, u][:], op0=ALU.mult, op1=ALU.add)
+
+        def turn(h, u):
+            turned[h, u] = psum.tile([P, PACK, P], F32, name="turned", tag="turned", bufs=TB_BUFS)
+            for t in range(PACK):
+                if h in ACC:
+                    nc.tensor.matmul(out=turned[h, u][:, t, :], lhsT=first[h, u][:, t, :], rhs=ident[:], start=True, stop=False, is_transpose=True)
+                    nc.tensor.matmul(out=turned[h, u][:, t, :], lhsT=both[h, u][:, t, :], rhs=ident[:], start=False, stop=True, is_transpose=True)
+                else:
+                    nc.tensor.transpose(out=turned[h, u][:, t, :], in_=both[h, u][:, t, :], identity=ident[:])
+
+        def add_memory(h, u):
+            j, g = steps[h]
+            if u == 0:
+                ys[h] = work.tile([P, PACK, H], F32, name="y", tag="y", bufs=4)
+                ybf[h] = work.tile([P, H, PACK], BF16, name="ybf", tag="ybf", bufs=2, align_bytes=64)
+            c0 = (j % 2) * H + u * P
+            nc.vector.tensor_tensor(out=ys[h][:, :, u * P:(u + 1) * P], in0=turned[h, u][:],
+                                    in1=raw["m", g, j // 2][:, :, c0:c0 + P], op=ALU.add)
+
+        def store_y(h, lo, hi):
+            j, g = steps[h]
+            nc.sync.dma_start(out=out_0[g * KP:(g + 1) * KP, j * H + lo:j * H + hi].rearrange("(p t) c -> p t c", t=PACK), in_=ys[h][:, :, lo:hi])
+
+        def quant_out(h, lo, hi):
+            j, g = steps[h]
+            if lo == 0:
+                words[h] = work.tile([P, H], U32, name="words", tag="words", bufs=4, align_bytes=64)
+            nc.vector.quantize_mx(out=words[h][:, lo:hi].bitcast(FP8X4), scales=out_scales[:, g, j * H + lo:j * H + hi],
+                                  in_=ybf[h][:, lo:hi, :].rearrange("p c t -> p (c t)"))
+
+        def store_words(h):
+            j, g = steps[h]
+            nc.sync.dma_start(out=out_1[g, :, j * H:(j + 1) * H, :].rearrange("p m t -> p (m t)").bitcast(I32), in_=words[h][:].bitcast(I32))
+
+        def store_scales(lo, hi, quads, eng):
+            for q in quads:
+                eng.dma_start(out=out_2[:, 4 * q:4 * q + 4, lo:hi].rearrange("g r m -> r g m").bitcast(I32),
+                                  in_=out_scales[32 * q:32 * q + 4, :, lo:hi].bitcast(I32))
+
+        out_scales = keep.tile([P, 2, F], U8, name="out_scales", align_bytes=64)
+        ident = keep.tile([P, P], F32, name="ident")
+        clip_rows = keep.tile([32, P], BF16, name="clip_rows")
+        clip_wide = keep.tile([P, P], F32, name="clip_wide")
+        clips = keep.tile([P, 32], F32, name="clips")
+        nc.scalar.dma_start(out=clip_rows[0:16, :], in_=clip_a.rearrange("(c p) -> c p", p=P))
+        nc.scalar.dma_start(out=clip_rows[16:32, :], in_=clip_b.rearrange("(c p) -> c p", p=P))
+        nc.gpsimd.memset(clip_wide[:], 0.0)
+        make_identity(nc, ident[:])
+        nc.scalar.activation(out=clip_wide[0:32, :], in_=clip_rows[:], func=ACT.Copy)
+        clip_psum = psum.tile([P, PACK, P], F32, name="turned", tag="turned", bufs=TB_BUFS)
+        nc.tensor.transpose(out=clip_psum[:, 0, :], in_=clip_wide[:], identity=ident[:])
+
+        n = len(steps)
+
+        def unit_loads(i):
+            u = units[i]
+            if u[0] == "x":
+                return [u]
+            r, j = u[1:]
+            return [("h", r, s, j) if j < 2 * SPLIT0 else ("z", r, s, j // 2) for s in range(2)]
+
+        def round_y(h, u, eng):
+            weave(eng, ybf[h][:, u * P:(u + 1) * P, :], ys[h][:, :, u * P:(u + 1) * P])
+
+        last = n - 1
+        sync_q, scalar_q, vector_q, gpsimd_q, tensor_q = [], [], [], [], []
+        done = 0
+        for h in range(n):
+            sync_q += [(key, [], load, (key,)) for key in loads[done:LP[h]]]
+            done = max(done, LP[h])
+            if h > 0:
+                sync_q.append((("sw", h - 1), [("qo", h - 1)], store_words, (h - 1,)))
+            if h == last - 1:
+                sync_q.append((("ss", 0), [("qo", n - 3)], store_scales, (0, F - H, range(4), nc.sync)))
+            if h < last:
+                sync_q.append((("sy", h), [("e", h, 1)], store_y, (h, 0, H)))
+        sync_q += [(("sy", last, u), [("e", last, u)], store_y, (last, u * P, (u + 1) * P)) for u in range(2)]
+        sync_q.append((("sw", last), [("qo", last)], store_words, (last,)))
+        sync_q.append((("ss", 1), [("qo", last)], store_scales, (F - H, F, range(2), nc.sync)))
+
+        helped = {}
+        for k in range(1, n + 1):
+            i = max(VP[:k + 1]) - 1 + STAGE_BUFS
+            if i < len(units) and i not in helped.values() and GS[i] > 0:
+                helped[k] = i
+        share = [W - (min(GS[i], W - VS[i]) if i in helped.values() else 0) for i in range(len(units))]
+
+        pieces = []
+        for i in range(len(units)):
+            mid = H if units[i][0] == "z" and VS[i] < H < share[i] else (VS[i] + share[i]) // 32 * 16
+            pieces += [(("ws", i, 0), unit_loads(i), weave_unit, (i, "S", VS[i], mid)),
+                       (("ws", i, 1), unit_loads(i), weave_unit, (i, "S", mid, share[i]))]
+        done = 0
+        for c in range(2 * n):
+            h, u = divmod(c, 2)
+            at = min(CP[c], len(pieces))
+            scalar_q += pieces[done:at]
+            done = max(done, at)
+            if h >= 2 and FENG[h - 2] == "S":
+                scalar_q.append((("f", h - 2, u), [("e", h - 2, u)], round_y, (h - 2, u, "S")))
+            scalar_q.append((("c", h, u), [("mm", h), "clips"], clip_first, (h, u)))
+            if h in ACC:
+                scalar_q.append((("d", h, u), [], clip_second, (h, u)))
+        scalar_q += pieces[done:]
+        if FENG[last - 1] == "S":
+            scalar_q += [(("f", last - 1, u), [("e", last - 1, u)], round_y, (last - 1, u, "S")) for u in range(2)]
+        scalar_q.append((("f", last, 0), [("e", last, 0)], round_y, (last, 0, "S")))
+        scalar_q.append((("ss", 2), [("qo", last)], store_scales, (F - H, F, range(2, 4), nc.scalar)))
+        scalar_q.insert(2, ("clips", [], lambda: nc.scalar.copy(out=clips[:], in_=clip_psum[:, 0, 0:32]), ()))
+
+        prep = [[(("wv", 0), unit_loads(0), weave_unit, (0, "V", 0, VS[0]))]] + [[] for i in units[1:]]
+        for i in range(len(units)):
+            if i + 1 < len(units):
+                prep[i].append((("wv", i + 1), unit_loads(i + 1), weave_unit, (i + 1, "V", 0, VS[i + 1])))
+            prep[i].append((("q",) + units[i], [("ws", i, 1)] + ([("wg", i)] if i in helped.values() else []), quant_in, (i,)))
+        done = 0
+        for k in range(n + 1):
+            part = []
+            for i in range(done, VP[k]):
+                part += prep[i]
+            done = max(done, VP[k])
+            if k >= 2:
+                part.insert(max(len(part) - QO_FIRST, 0), (("qo", k - 2), [("f", k - 2, 1)], quant_out, (k - 2, 0, H)))
+            vector_q += part
+            if k in helped:
+                i = helped[k]
+                gpsimd_q.append((("wg", i), unit_loads(i) + [("q",) + units[i - STAGE_BUFS]], weave_unit, (i, "G", share[i], W)))
+            if k >= 1:
+                j, g = steps[k - 1]
+                for u in range(2):
+                    vector_q.append((("e", k - 1, u), [("t", k - 1, u), ("m", g, j // 2)], add_memory, (k - 1, u)))
+                    if FENG[k - 1] == "G" and k - 1 < last:
+                        gpsimd_q.append((("f", k - 1, u), [("e", k - 1, u)], round_y, (k - 1, u, "G")))
+            if k < n and k not in ACC:
+                vector_q += [(("d", k, u), [("c", k, u)], clip_second, (k, u)) for u in range(2)]
+        vector_q.append((("f", last, 1), [], round_y, (last, 1, "V")))
+        vector_q.append((("qo", last, 0), [("f", last, 0)], quant_out, (last, 0, P)))
+        vector_q.append((("qo", last), [], quant_out, (last, P, H)))
+
+        for h in range(n + 1):
+            if h < n:
+                j, g = steps[h]
+                tensor_q.append((("mm", h), [("q", "z", 0, j), ("q", "z", 1, j)] + [("q", "x", r, s, g) for r in range(2) for s in range(2)], products, (h,)))
+            if h >= 1:
+                tensor_q += [(("t", h - 1, u), [("d", h - 1, u)], turn, (h - 1, u)) for u in range(2)]
+
+        written = set()
+        queues = [sync_q, scalar_q, vector_q, gpsimd_q, tensor_q]
+        heads = [0] * len(queues)
+        while any(heads[e] < len(q) for e, q in enumerate(queues)):
+            moved = False
+            for e, q in enumerate(queues):
+                while heads[e] < len(q) and all(k in written for k in q[heads[e]][1]):
+                    name, needs, call, args = q[heads[e]]
+                    call(*args)
+                    written.add(name)
+                    heads[e] += 1
+                    moved = True
+            assert moved

@@ -22,11 +22,11 @@ W = 512
 H = 256
 
 ORDER = [(0, 0), (1, 0), (0, 1), (1, 1)] + [(j, g) for j in range(2, 8) for g in range(2)]
-VS = [496, 304, 176, 400, 224, 400, 224, 208, 224, 400, 304, 272, 32, 0, 0, 16, 48, 48, 0, 0, 16, 0, 0, 0]
-VP = [10, 12, 11, 14, 15, 16, 14, 18, 19, 20, 21, 22, 23, 24, 24, 23, 24]
-CP = [13, 20, 26, 24, 22, 27, 28, 30, 27, 29, 32, 32, 34, 36, 31, 38, 38, 40, 41, 42, 44, 41, 42, 46, 50, 55, 46, 48, 48, 49, 57, 50]
-LP = [23, 25, 34, 34, 35, 36, 34, 36, 34, 36, 36, 35, 34, 34, 34, 36]
-FENG = "GGGGGGGGGGGGGGSS"
+VS = [336, 256, 208, 240, 272, 304, 320, 256, 352, 288, 208, 192, 240, 240, 240, 240, 240, 240, 240, 240, 240, 240, 240, 240]
+VP = [8, 12, 13, 14, 15, 16, 17, 18, 19, 20, 21, 22, 23, 24, 24, 24, 24]
+CP = [14, 18, 25, 24, 27, 27, 28, 27, 30, 29, 32, 31, 34, 33, 36, 35, 38, 37, 40, 39, 42, 41, 44, 43, 46, 45, 48, 47, 50, 49, 52, 51]
+LP = [29, 31, 33, 35, 36, 36, 36, 36, 36, 36, 36, 36, 36, 36, 36, 36]
+FENG = "SSSSSSSSSSSSSSSS"
 STAGE_BUFS = 4
 AB_BUFS = 3
 TB_BUFS = 2
@@ -35,7 +35,7 @@ GS = [0, 0, 0, 0, 0, 0, 0, 0, 0, 0, 0, 0, 0, 0, 0, 0, 0, 0, 0, 0, 0, 0, 0, 0]
 QO_FIRST = 0
 ACC = []
 A_BUFS = 3
-MP = [18, 21, 22, 22, 28, 34, 44, 35]
+MP = [16, 20, 23, 26, 31, 27, 38, 41]
 
 
 def tile_replica_weight_grad_g2_kernel(tc, xa, dza, xb, dzb, clip_a, clip_b, memory, out_0, out_1, out_2):

@@ -21,45 +21,40 @@ KP = P * PACK
 W = 512
 H = 256
 
-ORDER = [(0, 0), (1, 0), (0, 1), (1, 1)] + [(j, g) for j in range(2, 8) for g in range(2)]
-VS = [336, 256, 208, 240, 272, 304, 320, 256, 352, 288, 208, 192, 240, 240, 240, 240, 240, 240, 240, 240, 240, 240, 240, 240]
-VP = [8, 12, 13, 14, 15, 16, 17, 18, 19, 20, 21, 22, 23, 24, 24, 24, 24]
-CP = [14, 18, 25, 24, 27, 27, 28, 27, 30, 29, 32, 31, 34, 33, 36, 35, 38, 37, 40, 39, 42, 41, 44, 43, 46, 45, 48, 47, 50, 49, 52, 51]
-LP = [29, 31, 33, 35, 36, 36, 36, 36, 36, 36, 36, 36, 36, 36, 36, 36]
-FENG = "SSSSSSSSSSSSSSSS"
-STAGE_BUFS = 4
-AB_BUFS = 3
-TB_BUFS = 2
-SPLIT0 = 1
+ZC = [0, 512, 1024, 2048]
+MC = [0, 1024, 2048]
+HEAD = [0, 1, 2, 3, 8, 9, 4, 5, 6, 7, 10, 11]
+VS = [256, 256, 256, 256, 256, 256, 256, 256, 256, 256, 256, 256, 240, 240, 240, 240, 240, 240, 240, 240, 240, 240, 240, 240]
 GS = [0, 0, 0, 0, 0, 0, 0, 0, 0, 0, 0, 0, 0, 0, 0, 0, 0, 0, 0, 0, 0, 0, 0, 0]
+VP = [11, 12, 13, 14, 15, 16, 17, 18, 19, 20, 21, 22, 23, 24, 24, 24, 24]
+CP = [22, 22, 24, 24, 26, 26, 28, 28, 30, 30, 32, 32, 34, 34, 36, 36, 38, 38, 40, 40, 42, 42, 44, 44, 46, 46, 48, 48, 50, 50, 52, 52]
+LP = [18, 20, 20, 20, 20, 20, 20, 20]
+MP = [10, 13, 18, 19]
+STAGE_BUFS = 4
+BIG_BUFS = 7
+Y_BUFS = 4
+ZQ_BUFS = 5
 QO_FIRST = 0
-ACC = []
-A_BUFS = 3
-MP = [16, 20, 23, 26, 31, 27, 38, 41]
 
 
 def tile_replica_weight_grad_g2_kernel(tc, xa, dza, xb, dzb, clip_a, clip_b, memory, out_0, out_1, out_2):
     nc = tc.nc
     xs, dzs = (xa, xb), (dza, dzb)
-    steps = ORDER
-    units, loads = [], []
-    for j, g in steps:
-        for r in range(2):
-            for u in [("x", r, 0, g), ("x", r, 1, g), ("z", r, j)]:
-                if u not in units:
-                    units.append(u)
-                    if u[0] == "x":
-                        loads.append(u)
-                    elif j < 2 * SPLIT0:
-                        loads += [("h", r, 0, j), ("h", r, 1, j)]
-                    elif j % 2 == 0:
-                        loads += [("z", r, 0, j // 2), ("z", r, 1, j // 2)]
-    need = []
-    for j, g in steps:
-        if ("m", g, j // 2) not in need:
-            need.append(("m", g, j // 2))
-    for key, at in zip(need, MP):
+    steps = [(j, g) for j in range(8) for g in range(2)]
+    n = len(steps)
+    last = n - 1
+    first_units = [("x", r, s, g) for r in range(2) for s in range(2) for g in range(2)] + [("z", r, j) for r in range(2) for j in range(2)]
+    first_units = first_units[:8] + [first_units[8], first_units[9], first_units[10], first_units[11]]
+    units = [first_units[i] for i in HEAD] + [("z", r, j) for j in range(2, 8) for r in range(2)]
+    loads = []
+    for r in range(2):
+        loads += [("x", r, 0), ("x", r, 1), ("z", r, 0, 0), ("z", r, 1, 0)]
+    loads += [("z", r, s, c) for c in range(1, len(ZC) - 1) for r in range(2) for s in range(2)]
+    for key, at in zip([("m", g, c) for c in range(len(MC) - 1) for g in range(2)], MP):
         loads.insert(at, key)
+
+    def chunk(cuts, col):
+        return max(c for c in range(len(cuts) - 1) if cuts[c] <= col)
 
     with ExitStack() as ctx:
         keep = ctx.enter_context(tc.tile_pool(name="keep", bufs=1))
@@ -71,20 +66,19 @@ def tile_replica_weight_grad_g2_kernel(tc, xa, dza, xb, dzb, clip_a, clip_b, mem
 
         def load(key):
             if key[0] == "m":
-                g, q = key[1:]
-                src, tag, bufs = memory[g * KP:(g + 1) * KP, q * W:(q + 1) * W], "mem", 8
-            elif key[0] == "h":
-                r, s, c = key[1:]
-                src, tag, bufs = dzs[r][s * KP:(s + 1) * KP, c * H:(c + 1) * H], "half", 8 * SPLIT0
+                g, c = key[1:]
+                src, tag, bufs = memory[g * KP:(g + 1) * KP, MC[c]:MC[c + 1]], "mem%d" % c, 2
+            elif key[0] == "x":
+                r, s = key[1:]
+                src, tag, bufs = xs[r][s * KP:(s + 1) * KP, :], "big", BIG_BUFS
             else:
                 r, s, c = key[1:]
-                src, tag, bufs = (xs if key[0] == "x" else dzs)[r][s * KP:(s + 1) * KP, c * W:(c + 1) * W], "raw", 24 - 4 * SPLIT0
+                src = dzs[r][s * KP:(s + 1) * KP, ZC[c]:ZC[c + 1]]
+                tag, bufs = ("big", BIG_BUFS) if src.shape[1] == D else ("z%d" % c, 4)
             raw[key] = work.tile([P, PACK, src.shape[1]], BF16, name=tag, tag=tag, bufs=bufs)
             nc.sync.dma_start(out=raw[key][:], in_=src.rearrange("(p t) c -> p t c", t=PACK))
 
-        def weave(eng, dst, src):
-            dst = dst.rearrange("p (c i) t -> p c t i", i=4)
-            src = src.rearrange("p t (c i) -> p c t i", i=4)
+        def copy_on(eng, dst, src):
             if eng == "V":
                 nc.vector.tensor_copy(out=dst, in_=src)
             elif eng == "S":
@@ -92,27 +86,37 @@ def tile_replica_weight_grad_g2_kernel(tc, xa, dza, xb, dzb, clip_a, clip_b, mem
             else:
                 nc.gpsimd.tensor_scalar(out=dst, in0=src, scalar1=1.0, scalar2=0.0, op0=ALU.mult, op1=ALU.add)
 
+        def weave(eng, dst, src):
+            if eng == "G":
+                copy_on(eng, dst, src.rearrange("p t c -> p c t"))
+            else:
+                copy_on(eng, dst.rearrange("p (c i) t -> p c t i", i=4), src.rearrange("p t (c i) -> p c t i", i=4))
+
+        def unit_loads(i):
+            u = units[i]
+            if u[0] == "x":
+                return [u[:3]]
+            return [("z", u[1], s, chunk(ZC, u[2] * H)) for s in range(2)]
+
         def weave_unit(i, eng, lo, hi):
             u = units[i]
             if i not in stage:
                 stage[i] = work.tile([P, W, PACK], BF16, name="stage", tag="stage%d" % (i % STAGE_BUFS), bufs=1, align_bytes=64)
             if u[0] == "x":
                 if hi > lo:
-                    weave(eng, stage[i][:, lo:hi, :], raw[u][:, :, lo:hi])
+                    dst = stage[i][:].rearrange("p (e m) t -> p m t e", e=PACK)
+                    src = raw[u[:3]][:, :, u[3] * W:(u[3] + 1) * W].rearrange("p t (m e) -> p m t e", e=PACK)
+                    copy_on(eng, dst[:, lo // PACK:hi // PACK, :, :], src[:, lo // PACK:hi // PACK, :, :])
                 return
-            r, j = u[1:]
-            for s in range(2):
+            for s, key in enumerate(unit_loads(i)):
                 a, b = max(lo, s * H), min(hi, (s + 1) * H)
                 if b > a:
-                    if j < 2 * SPLIT0:
-                        src, off = raw["h", r, s, j], -s * H
-                    else:
-                        src, off = raw["z", r, s, j // 2], (j % 2) * H - s * H
-                    weave(eng, stage[i][:, a:b, :], src[:, :, a + off:b + off])
+                    off = u[2] * H - ZC[key[3]] - s * H
+                    weave(eng, stage[i][:, a:b, :], raw[key][:, :, a + off:b + off])
 
         def quant_in(i):
             u = units[i]
-            tag, bufs = ("xq", 8) if u[0] == "x" else ("zq", 6)
+            tag, bufs = ("xq", 8) if u[0] == "x" else ("zq", ZQ_BUFS)
             codes[u] = work.tile([P, W], U32, name=tag + "c", tag=tag + "c", bufs=bufs, align_bytes=64)
             scales[u] = work.tile([P, W], U8, name=tag + "s", tag=tag + "s", bufs=bufs, align_bytes=64)
             nc.vector.quantize_mx(out=codes[u][:].bitcast(FP8X4), scales=scales[u][:], in_=stage[i][:].rearrange("p c t -> p (c t)"))
@@ -121,7 +125,7 @@ def tile_replica_weight_grad_g2_kernel(tc, xa, dza, xb, dzb, clip_a, clip_b, mem
             j, g = steps[h]
             for u in range(2):
                 for r in range(2):
-                    banks[h, u, r] = psum.tile([P, W], F32, name="ab"[r], tag="ab"[r], bufs=(A_BUFS, AB_BUFS)[r])
+                    banks[h, u, r] = psum.tile([P, W], F32, name="ab"[r], tag="ab"[r], bufs=3)
                     for s in range(2):
                         cols = slice(s * H + u * P, s * H + (u + 1) * P)
                         nc.tensor.matmul_mx(
@@ -132,57 +136,55 @@ def tile_replica_weight_grad_g2_kernel(tc, xa, dza, xb, dzb, clip_a, clip_b, mem
 
         def clip_first(h, u):
             c = 2 * steps[h][0] + u
-            first[h, u] = work.tile([P, PACK, P], F32, name="first", tag="first", bufs=4)
-            nc.scalar.activation(out=first[h, u][:], in_=banks[h, u, 0][:].rearrange("p (m t) -> p t m", t=PACK),
-                                 func=ACT.Copy, scale=clips[:, c:c + 1])
+            first[h, u] = work.tile([P, W], F32, name="first", tag="first", bufs=4)
+            nc.scalar.activation(out=first[h, u][:], in_=banks[h, u, 0][:], func=ACT.Copy, scale=clips[:, c:c + 1])
 
         def clip_second(h, u):
             c = 16 + 2 * steps[h][0] + u
-            both[h, u] = work.tile([P, PACK, P], F32, name="both", tag="both", bufs=4)
-            if h in ACC:
-                nc.scalar.activation(out=both[h, u][:], in_=banks[h, u, 1][:].rearrange("p (m t) -> p t m", t=PACK),
-                                     func=ACT.Copy, scale=clips[:, c:c + 1])
-                return
-            nc.vector.scalar_tensor_tensor(out=both[h, u][:], in0=banks[h, u, 1][:].rearrange("p (m t) -> p t m", t=PACK),
+            both[h, u] = work.tile([P, W], F32, name="both", tag="both", bufs=4)
+            nc.vector.scalar_tensor_tensor(out=both[h, u][:], in0=banks[h, u, 1][:],
                                            scalar=clips[:, c:c + 1], in1=first[h, u][:], op0=ALU.mult, op1=ALU.add)
 
         def turn(h, u):
-            turned[h, u] = psum.tile([P, PACK, P], F32, name="turned", tag="turned", bufs=TB_BUFS)
+            turned[h, u] = psum.tile([P, PACK, P], F32, name="turned", tag="turned", bufs=2)
             for t in range(PACK):
-                if h in ACC:
-                    nc.tensor.matmul(out=turned[h, u][:, t, :], lhsT=first[h, u][:, t, :], rhs=ident[:], start=True, stop=False, is_transpose=True)
-                    nc.tensor.matmul(out=turned[h, u][:, t, :], lhsT=both[h, u][:, t, :], rhs=ident[:], start=False, stop=True, is_transpose=True)
-                else:
-                    nc.tensor.transpose(out=turned[h, u][:, t, :], in_=both[h, u][:, t, :], identity=ident[:])
+                nc.tensor.transpose(out=turned[h, u][:, t, :], in_=both[h, u][:, t * P:(t + 1) * P], identity=ident[:])
 
         def add_memory(h, u):
             j, g = steps[h]
             if u == 0:
-                ys[h] = work.tile([P, PACK, H], F32, name="y", tag="y", bufs=4)
                 ybf[h] = work.tile([P, H, PACK], BF16, name="ybf", tag="ybf", bufs=2, align_bytes=64)
-            c0 = (j % 2) * H + u * P
-            nc.vector.tensor_tensor(out=ys[h][:, :, u * P:(u + 1) * P], in0=turned[h, u][:],
-                                    in1=raw["m", g, j // 2][:, :, c0:c0 + P], op=ALU.add)
+                if j % 2 == 0:
+                    ys[j // 2, g] = work.tile([P, PACK, W], F32, name="y", tag="y", bufs=Y_BUFS)
+            c = chunk(MC, j * H)
+            c0 = j * H + u * P - MC[c]
+            y0 = (j % 2) * H + u * P
+            nc.vector.tensor_tensor(out=ys[j // 2, g][:, :, y0:y0 + P], in0=turned[h, u][:],
+                                    in1=raw["m", g, c][:, :, c0:c0 + P], op=ALU.add)
 
-        def store_y(h, lo, hi):
+        def round_y(h, u, eng):
             j, g = steps[h]
-            nc.sync.dma_start(out=out_0[g * KP:(g + 1) * KP, j * H + lo:j * H + hi].rearrange("(p t) c -> p t c", t=PACK), in_=ys[h][:, :, lo:hi])
+            y0 = (j % 2) * H + u * P
+            weave(eng, ybf[h][:, u * P:(u + 1) * P, :], ys[j // 2, g][:, :, y0:y0 + P])
 
         def quant_out(h, lo, hi):
             j, g = steps[h]
-            if lo == 0:
-                words[h] = work.tile([P, H], U32, name="words", tag="words", bufs=4, align_bytes=64)
-            nc.vector.quantize_mx(out=words[h][:, lo:hi].bitcast(FP8X4), scales=out_scales[:, g, j * H + lo:j * H + hi],
+            if lo == 0 and j % 2 == 0:
+                words[j // 2, g] = work.tile([P, W], U32, name="words", tag="words", bufs=4, align_bytes=64)
+            y0 = (j % 2) * H
+            nc.vector.quantize_mx(out=words[j // 2, g][:, y0 + lo:y0 + hi].bitcast(FP8X4), scales=out_scales[:, g, j * H + lo:j * H + hi],
                                   in_=ybf[h][:, lo:hi, :].rearrange("p c t -> p (c t)"))
 
-        def store_words(h):
-            j, g = steps[h]
-            nc.sync.dma_start(out=out_1[g, :, j * H:(j + 1) * H, :].rearrange("p m t -> p (m t)").bitcast(I32), in_=words[h][:].bitcast(I32))
+        def store_y(q, g, lo, hi):
+            nc.sync.dma_start(out=out_0[g * KP:(g + 1) * KP, q * W + lo:q * W + hi].rearrange("(p t) c -> p t c", t=PACK), in_=ys[q, g][:, :, lo:hi])
+
+        def store_words(q, g, lo, hi):
+            nc.sync.dma_start(out=out_1[g, :, q * W + lo:q * W + hi, :].rearrange("p m t -> p (m t)").bitcast(I32), in_=words[q, g][:, lo:hi].bitcast(I32))
 
         def store_scales(lo, hi, quads, eng):
             for q in quads:
                 eng.dma_start(out=out_2[:, 4 * q:4 * q + 4, lo:hi].rearrange("g r m -> r g m").bitcast(I32),
-                                  in_=out_scales[32 * q:32 * q + 4, :, lo:hi].bitcast(I32))
+                              in_=out_scales[32 * q:32 * q + 4, :, lo:hi].bitcast(I32))
 
         out_scales = keep.tile([P, 2, F], U8, name="out_scales", align_bytes=64)
         ident = keep.tile([P, P], F32, name="ident")
@@ -194,36 +196,25 @@ def tile_replica_weight_grad_g2_kernel(tc, xa, dza, xb, dzb, clip_a, clip_b, mem
         nc.gpsimd.memset(clip_wide[:], 0.0)
         make_identity(nc, ident[:])
         nc.scalar.activation(out=clip_wide[0:32, :], in_=clip_rows[:], func=ACT.Copy)
-        clip_psum = psum.tile([P, PACK, P], F32, name="turned", tag="turned", bufs=TB_BUFS)
+        clip_psum = psum.tile([P, PACK, P], F32, name="turned", tag="turned", bufs=2)
         nc.tensor.transpose(out=clip_psum[:, 0, :], in_=clip_wide[:], identity=ident[:])
 
-        n = len(steps)
-
-        def unit_loads(i):
-            u = units[i]
-            if u[0] == "x":
-                return [u]
-            r, j = u[1:]
-            return [("h", r, s, j) if j < 2 * SPLIT0 else ("z", r, s, j // 2) for s in range(2)]
-
-        def round_y(h, u, eng):
-            weave(eng, ybf[h][:, u * P:(u + 1) * P, :], ys[h][:, :, u * P:(u + 1) * P])
-
-        last = n - 1
         sync_q, scalar_q, vector_q, gpsimd_q, tensor_q = [], [], [], [], []
         done = 0
-        for h in range(n):
-            sync_q += [(key, [], load, (key,)) for key in loads[done:LP[h]]]
-            done = max(done, LP[h])
-            if h > 0:
-                sync_q.append((("sw", h - 1), [("qo", h - 1)], store_words, (h - 1,)))
-            if h == last - 1:
-                sync_q.append((("ss", 0), [("qo", n - 3)], store_scales, (0, F - H, range(4), nc.sync)))
-            if h < last:
-                sync_q.append((("sy", h), [("e", h, 1)], store_y, (h, 0, H)))
-        sync_q += [(("sy", last, u), [("e", last, u)], store_y, (last, u * P, (u + 1) * P)) for u in range(2)]
-        sync_q.append((("sw", last), [("qo", last)], store_words, (last,)))
-        sync_q.append((("ss", 1), [("qo", last)], store_scales, (F - H, F, range(2), nc.sync)))
+        stores = []
+        for h, (j, g) in enumerate(steps):
+            if j % 2 == 1 or j == 6:
+                lo, hi = (0, W) if j < 6 else ((j - 6) * H, (j - 5) * H)
+                stores.append((("sy", h), [("e", h, 1)], store_y, (j // 2, g, lo, hi)))
+                stores.append((("sw", h), [("qo", h)], store_words, (j // 2, g, lo, hi)))
+            if h == last - 2:
+                stores.append((("ss", 0), [], store_scales, (0, F - H, range(4), nc.sync)))
+        stores.append((("ss", 1), [("qo", last)], store_scales, (F - H, F, range(2), nc.sync)))
+        for b, store in enumerate(stores):
+            at = min(LP[b], len(loads)) if b < len(LP) else len(loads)
+            sync_q += [(key, [], load, (key,)) for key in loads[done:at]]
+            done = max(done, at)
+            sync_q.append(store)
 
         helped = {}
         for k in range(1, n + 1):
@@ -243,14 +234,11 @@ def tile_replica_weight_grad_g2_kernel(tc, xa, dza, xb, dzb, clip_a, clip_b, mem
             at = min(CP[c], len(pieces))
             scalar_q += pieces[done:at]
             done = max(done, at)
-            if h >= 2 and FENG[h - 2] == "S":
+            if h >= 2:
                 scalar_q.append((("f", h - 2, u), [("e", h - 2, u)], round_y, (h - 2, u, "S")))
             scalar_q.append((("c", h, u), [("mm", h), "clips"], clip_first, (h, u)))
-            if h in ACC:
-                scalar_q.append((("d", h, u), [], clip_second, (h, u)))
         scalar_q += pieces[done:]
-        if FENG[last - 1] == "S":
-            scalar_q += [(("f", last - 1, u), [("e", last - 1, u)], round_y, (last - 1, u, "S")) for u in range(2)]
+        scalar_q += [(("f", last - 1, u), [("e", last - 1, u)], round_y, (last - 1, u, "S")) for u in range(2)]
         scalar_q.append((("f", last, 0), [("e", last, 0)], round_y, (last, 0, "S")))
         scalar_q.append((("ss", 2), [("qo", last)], store_scales, (F - H, F, range(2, 4), nc.scalar)))
         scalar_q.insert(2, ("clips", [], lambda: nc.scalar.copy(out=clips[:], in_=clip_psum[:, 0, 0:32]), ()))
@@ -275,10 +263,8 @@ def tile_replica_weight_grad_g2_kernel(tc, xa, dza, xb, dzb, clip_a, clip_b, mem
             if k >= 1:
                 j, g = steps[k - 1]
                 for u in range(2):
-                    vector_q.append((("e", k - 1, u), [("t", k - 1, u), ("m", g, j // 2)], add_memory, (k - 1, u)))
-                    if FENG[k - 1] == "G" and k - 1 < last:
-                        gpsimd_q.append((("f", k - 1, u), [("e", k - 1, u)], round_y, (k - 1, u, "G")))
-            if k < n and k not in ACC:
+                    vector_q.append((("e", k - 1, u), [("t", k - 1, u), ("m", g, chunk(MC, j * H))], add_memory, (k - 1, u)))
+            if k < n:
                 vector_q += [(("d", k, u), [("c", k, u)], clip_second, (k, u)) for u in range(2)]
         vector_q.append((("f", last, 1), [], round_y, (last, 1, "V")))
         vector_q.append((("qo", last, 0), [("f", last, 0)], quant_out, (last, 0, P)))

@@ -21,19 +21,27 @@ KP = P * PACK
 W = 512
 H = 256
 
+XH = [0, 0, 0, 0]
+LO = [0, 2, 8, 9, 4, 6, 10, 11]
+G0 = 0
 ZC = [0, 512, 1024, 2048]
 MC = [0, 1024, 2048]
-HEAD = [0, 1, 2, 3, 8, 9, 4, 5, 6, 7, 10, 11]
-VS = [256, 256, 256, 256, 256, 256, 256, 256, 256, 256, 256, 256, 240, 240, 240, 240, 240, 240, 240, 240, 240, 240, 240, 240]
-GS = [0, 0, 0, 0, 0, 0, 0, 0, 0, 0, 0, 0, 0, 0, 0, 0, 0, 0, 0, 0, 0, 0, 0, 0]
+HEAD = [0, 1, 2, 3, 8, 9, 4, 5, 6, 10, 7, 11]
+VS = [272, 272, 272, 272, 272, 272, 272, 272, 272, 272, 272, 272, 192, 192, 64, 64, 64, 64, 64, 64, 64, 64, 64, 64]
+GS = [0, 0, 0, 0, 0, 0, 0, 0, 0, 0, 0, 0, 0, 0, 256, 256, 256, 256, 256, 256, 256, 256, 256, 256]
 VP = [11, 12, 13, 14, 15, 16, 17, 18, 19, 20, 21, 22, 23, 24, 24, 24, 24]
-CP = [22, 22, 24, 24, 26, 26, 28, 28, 30, 30, 32, 32, 34, 34, 36, 36, 38, 38, 40, 40, 42, 42, 44, 44, 46, 46, 48, 48, 50, 50, 52, 52]
-LP = [18, 20, 20, 20, 20, 20, 20, 20]
+CP = [18, 18, 22, 24, 26, 27, 28, 29, 30, 31, 32, 33, 34, 35, 36, 37, 38, 39, 40, 41, 42, 43, 44, 45, 46, 47, 48, 49, 50, 51, 52, 53]
+LP = [20, 20, 20, 20, 20, 20, 20, 20]
 MP = [10, 13, 18, 19]
 STAGE_BUFS = 4
 BIG_BUFS = 7
 Y_BUFS = 4
 ZQ_BUFS = 5
+FL = 3
+QL = 3
+FU = 0
+YB_BUFS = 3
+GB = 2
 QO_FIRST = 0
 
 
@@ -41,14 +49,15 @@ def tile_replica_weight_grad_g2_kernel(tc, xa, dza, xb, dzb, clip_a, clip_b, mem
     nc = tc.nc
     xs, dzs = (xa, xb), (dza, dzb)
     steps = [(j, g) for j in range(8) for g in range(2)]
+    if G0:
+        steps[1], steps[2] = steps[2], steps[1]
     n = len(steps)
     last = n - 1
     first_units = [("x", r, s, g) for r in range(2) for s in range(2) for g in range(2)] + [("z", r, j) for r in range(2) for j in range(2)]
     first_units = first_units[:8] + [first_units[8], first_units[9], first_units[10], first_units[11]]
     units = [first_units[i] for i in HEAD] + [("z", r, j) for j in range(2, 8) for r in range(2)]
-    loads = []
-    for r in range(2):
-        loads += [("x", r, 0), ("x", r, 1), ("z", r, 0, 0), ("z", r, 1, 0)]
+    early = [("x", r, s, g) for r in range(2) for s in range(2) for g in range(2)] + [("z", r, s, 0) for r in range(2) for s in range(2)]
+    loads = [early[i] for i in LO]
     loads += [("z", r, s, c) for c in range(1, len(ZC) - 1) for r in range(2) for s in range(2)]
     for key, at in zip([("m", g, c) for c in range(len(MC) - 1) for g in range(2)], MP):
         loads.insert(at, key)
@@ -69,8 +78,11 @@ def tile_replica_weight_grad_g2_kernel(tc, xa, dza, xb, dzb, clip_a, clip_b, mem
                 g, c = key[1:]
                 src, tag, bufs = memory[g * KP:(g + 1) * KP, MC[c]:MC[c + 1]], "mem%d" % c, 2
             elif key[0] == "x":
-                r, s = key[1:]
-                src, tag, bufs = xs[r][s * KP:(s + 1) * KP, :], "big", BIG_BUFS
+                r, s, g = key[1:]
+                if XH[2 * r + s]:
+                    src, tag, bufs = xs[r][s * KP:(s + 1) * KP, g * W:(g + 1) * W], "xh", 2 * sum(XH)
+                else:
+                    src, tag, bufs = xs[r][s * KP:(s + 1) * KP, :], "big", BIG_BUFS
             else:
                 r, s, c = key[1:]
                 src = dzs[r][s * KP:(s + 1) * KP, ZC[c]:ZC[c + 1]]
@@ -95,17 +107,18 @@ def tile_replica_weight_grad_g2_kernel(tc, xa, dza, xb, dzb, clip_a, clip_b, mem
         def unit_loads(i):
             u = units[i]
             if u[0] == "x":
-                return [u[:3]]
+                return [u if XH[2 * u[1] + u[2]] else u[:3] + (0,)]
             return [("z", u[1], s, chunk(ZC, u[2] * H)) for s in range(2)]
 
         def weave_unit(i, eng, lo, hi):
             u = units[i]
             if i not in stage:
-                stage[i] = work.tile([P, W, PACK], BF16, name="stage", tag="stage%d" % (i % STAGE_BUFS), bufs=1, align_bytes=64)
+                stage[i] = work.tile([P, W, PACK], BF16, name="stage", tag="stage%d" % (i % (STAGE_BUFS if i < 12 else GB)), bufs=1, align_bytes=64)
             if u[0] == "x":
                 if hi > lo:
                     dst = stage[i][:].rearrange("p (e m) t -> p m t e", e=PACK)
-                    src = raw[u[:3]][:, :, u[3] * W:(u[3] + 1) * W].rearrange("p t (m e) -> p m t e", e=PACK)
+                    g0 = 0 if XH[2 * u[1] + u[2]] else u[3] * W
+                    src = raw[unit_loads(i)[0]][:, :, g0:g0 + W].rearrange("p t (m e) -> p m t e", e=PACK)
                     copy_on(eng, dst[:, lo // PACK:hi // PACK, :, :], src[:, lo // PACK:hi // PACK, :, :])
                 return
             for s, key in enumerate(unit_loads(i)):
@@ -121,18 +134,16 @@ def tile_replica_weight_grad_g2_kernel(tc, xa, dza, xb, dzb, clip_a, clip_b, mem
             scales[u] = work.tile([P, W], U8, name=tag + "s", tag=tag + "s", bufs=bufs, align_bytes=64)
             nc.vector.quantize_mx(out=codes[u][:].bitcast(FP8X4), scales=scales[u][:], in_=stage[i][:].rearrange("p c t -> p (c t)"))
 
-        def products(h):
+        def product(h, u, r):
             j, g = steps[h]
-            for u in range(2):
-                for r in range(2):
-                    banks[h, u, r] = psum.tile([P, W], F32, name="ab"[r], tag="ab"[r], bufs=3)
-                    for s in range(2):
-                        cols = slice(s * H + u * P, s * H + (u + 1) * P)
-                        nc.tensor.matmul_mx(
-                            out=banks[h, u, r][:],
-                            lhsT=codes["z", r, j][:, cols].bitcast(FP8X4), lhsT_scale=scales["z", r, j][:, cols],
-                            rhs=codes["x", r, s, g][:].bitcast(FP8X4), rhs_scale=scales["x", r, s, g][:],
-                            start=(s == 0), stop=(s == 1))
+            banks[h, u, r] = psum.tile([P, W], F32, name="ab"[r], tag="ab"[r], bufs=3)
+            for s in range(2):
+                cols = slice(s * H + u * P, s * H + (u + 1) * P)
+                nc.tensor.matmul_mx(
+                    out=banks[h, u, r][:],
+                    lhsT=codes["z", r, j][:, cols].bitcast(FP8X4), lhsT_scale=scales["z", r, j][:, cols],
+                    rhs=codes["x", r, s, g][:].bitcast(FP8X4), rhs_scale=scales["x", r, s, g][:],
+                    start=(s == 0), stop=(s == 1))
 
         def clip_first(h, u):
             c = 2 * steps[h][0] + u
@@ -153,7 +164,6 @@ def tile_replica_weight_grad_g2_kernel(tc, xa, dza, xb, dzb, clip_a, clip_b, mem
         def add_memory(h, u):
             j, g = steps[h]
             if u == 0:
-                ybf[h] = work.tile([P, H, PACK], BF16, name="ybf", tag="ybf", bufs=2, align_bytes=64)
                 if j % 2 == 0:
                     ys[j // 2, g] = work.tile([P, PACK, W], F32, name="y", tag="y", bufs=Y_BUFS)
             c = chunk(MC, j * H)
@@ -162,10 +172,12 @@ def tile_replica_weight_grad_g2_kernel(tc, xa, dza, xb, dzb, clip_a, clip_b, mem
             nc.vector.tensor_tensor(out=ys[j // 2, g][:, :, y0:y0 + P], in0=turned[h, u][:],
                                     in1=raw["m", g, c][:, :, c0:c0 + P], op=ALU.add)
 
-        def round_y(h, u, eng):
+        def round_y(h, lo, hi, eng):
             j, g = steps[h]
-            y0 = (j % 2) * H + u * P
-            weave(eng, ybf[h][:, u * P:(u + 1) * P, :], ys[j // 2, g][:, :, y0:y0 + P])
+            if h not in ybf:
+                ybf[h] = work.tile([P, H, PACK], BF16, name="ybf", tag="ybf", bufs=YB_BUFS, align_bytes=64)
+            y0 = (j % 2) * H
+            weave(eng, ybf[h][:, lo:hi, :], ys[j // 2, g][:, :, y0 + lo:y0 + hi])
 
         def quant_out(h, lo, hi):
             j, g = steps[h]
@@ -193,23 +205,26 @@ def tile_replica_weight_grad_g2_kernel(tc, xa, dza, xb, dzb, clip_a, clip_b, mem
         clips = keep.tile([P, 32], F32, name="clips")
         nc.scalar.dma_start(out=clip_rows[0:16, :], in_=clip_a.rearrange("(c p) -> c p", p=P))
         nc.scalar.dma_start(out=clip_rows[16:32, :], in_=clip_b.rearrange("(c p) -> c p", p=P))
-        nc.gpsimd.memset(clip_wide[:], 0.0)
         make_identity(nc, ident[:])
-        nc.scalar.activation(out=clip_wide[0:32, :], in_=clip_rows[:], func=ACT.Copy)
+        nc.scalar.activation(out=clip_wide[:], in_=ident[:], func=ACT.Copy, scale=0.0)
         clip_psum = psum.tile([P, PACK, P], F32, name="turned", tag="turned", bufs=2)
-        nc.tensor.transpose(out=clip_psum[:, 0, :], in_=clip_wide[:], identity=ident[:])
+
+        def widen_clips():
+            nc.scalar.copy(out=clip_wide[0:32, :], in_=clip_rows[:])
+            nc.tensor.transpose(out=clip_psum[:, 0, :], in_=clip_wide[:], identity=ident[:])
 
         sync_q, scalar_q, vector_q, gpsimd_q, tensor_q = [], [], [], [], []
         done = 0
         stores = []
-        for h, (j, g) in enumerate(steps):
-            if j % 2 == 1 or j == 6:
-                lo, hi = (0, W) if j < 6 else ((j - 6) * H, (j - 5) * H)
-                stores.append((("sy", h), [("e", h, 1)], store_y, (j // 2, g, lo, hi)))
-                stores.append((("sw", h), [("qo", h)], store_words, (j // 2, g, lo, hi)))
-            if h == last - 2:
-                stores.append((("ss", 0), [], store_scales, (0, F - H, range(4), nc.sync)))
-        stores.append((("ss", 1), [("qo", last)], store_scales, (F - H, F, range(2), nc.sync)))
+        for k in range(1, n + QL + 1):
+            for h, kind, call in ((k - QL, "qo", store_words), (k - 1, "e", store_y)):
+                if 0 <= h < n and (steps[h][0] % 2 == 1 or steps[h][0] == 6):
+                    j, g = steps[h]
+                    lo, hi = (0, W) if j < 6 else ((j - 6) * H, (j - 5) * H)
+                    stores.append(((kind + "s", h), [("qo", h) if kind == "qo" else ("e", h, 1)], call, (j // 2, g, lo, hi)))
+            if k - QL == last - 4:
+                stores.append((("ss", 0), [], store_scales, (0, F - W, range(4), nc.sync)))
+        stores.append((("ss", 1), [("qo", last)], store_scales, (F - W, F, range(2), nc.sync)))
         for b, store in enumerate(stores):
             at = min(LP[b], len(loads)) if b < len(LP) else len(loads)
             sync_q += [(key, [], load, (key,)) for key in loads[done:at]]
@@ -218,7 +233,7 @@ def tile_replica_weight_grad_g2_kernel(tc, xa, dza, xb, dzb, clip_a, clip_b, mem
 
         helped = {}
         for k in range(1, n + 1):
-            i = max(VP[:k + 1]) - 1 + STAGE_BUFS
+            i = max(VP[:k + 1]) - 1 + GB
             if i < len(units) and i not in helped.values() and GS[i] > 0:
                 helped[k] = i
         share = [W - (min(GS[i], W - VS[i]) if i in helped.values() else 0) for i in range(len(units))]
@@ -234,14 +249,15 @@ def tile_replica_weight_grad_g2_kernel(tc, xa, dza, xb, dzb, clip_a, clip_b, mem
             at = min(CP[c], len(pieces))
             scalar_q += pieces[done:at]
             done = max(done, at)
-            if h >= 2:
-                scalar_q.append((("f", h - 2, u), [("e", h - 2, u)], round_y, (h - 2, u, "S")))
-            scalar_q.append((("c", h, u), [("mm", h), "clips"], clip_first, (h, u)))
+            if h >= FL and u == FU:
+                scalar_q.append((("f", h - FL), [("e", h - FL, 1)], round_y, (h - FL, 0, H, "S")))
+            scalar_q.append((("c", h, u), [("mm", h, u, 0), "clips"], clip_first, (h, u)))
         scalar_q += pieces[done:]
-        scalar_q += [(("f", last - 1, u), [("e", last - 1, u)], round_y, (last - 1, u, "S")) for u in range(2)]
-        scalar_q.append((("f", last, 0), [("e", last, 0)], round_y, (last, 0, "S")))
-        scalar_q.append((("ss", 2), [("qo", last)], store_scales, (F - H, F, range(2, 4), nc.scalar)))
-        scalar_q.insert(2, ("clips", [], lambda: nc.scalar.copy(out=clips[:], in_=clip_psum[:, 0, 0:32]), ()))
+        scalar_q += [(("f", h), [("e", h, 1)], round_y, (h, 0, H, "S")) for h in range(n - FL, last)]
+        scalar_q.append((("f", last, 0), [("e", last, 0)], round_y, (last, 0, P, "S")))
+        scalar_q.append((("ss", 2), [("qo", last)], store_scales, (F - W, F, range(2, 4), nc.scalar)))
+        scalar_q.insert(4, ("widen", [], widen_clips, ()))
+        scalar_q.insert(7, ("clips", [], lambda: nc.scalar.copy(out=clips[:], in_=clip_psum[:, 0, 0:32]), ()))
 
         prep = [[(("wv", 0), unit_loads(0), weave_unit, (0, "V", 0, VS[0]))]] + [[] for i in units[1:]]
         for i in range(len(units)):
@@ -254,26 +270,28 @@ def tile_replica_weight_grad_g2_kernel(tc, xa, dza, xb, dzb, clip_a, clip_b, mem
             for i in range(done, VP[k]):
                 part += prep[i]
             done = max(done, VP[k])
-            if k >= 2:
-                part.insert(max(len(part) - QO_FIRST, 0), (("qo", k - 2), [("f", k - 2, 1)], quant_out, (k - 2, 0, H)))
+            if k >= QL:
+                part.insert(max(len(part) - QO_FIRST, 0), (("qo", k - QL), [("f", k - QL)], quant_out, (k - QL, 0, H)))
             vector_q += part
             if k in helped:
                 i = helped[k]
-                gpsimd_q.append((("wg", i), unit_loads(i) + [("q",) + units[i - STAGE_BUFS]], weave_unit, (i, "G", share[i], W)))
+                gpsimd_q.append((("wg", i), unit_loads(i) + [("q",) + units[i - GB]], weave_unit, (i, "G", share[i], W)))
             if k >= 1:
                 j, g = steps[k - 1]
                 for u in range(2):
                     vector_q.append((("e", k - 1, u), [("t", k - 1, u), ("m", g, chunk(MC, j * H))], add_memory, (k - 1, u)))
             if k < n:
-                vector_q += [(("d", k, u), [("c", k, u)], clip_second, (k, u)) for u in range(2)]
-        vector_q.append((("f", last, 1), [], round_y, (last, 1, "V")))
+                vector_q += [(("d", k, u), [("c", k, u), ("mm", k, u, 1)], clip_second, (k, u)) for u in range(2)]
+        vector_q += [(("qo", h), [("f", h)], quant_out, (h, 0, H)) for h in range(n + 1 - QL, last)]
+        vector_q.append((("f", last, 1), [], round_y, (last, P, H, "V")))
         vector_q.append((("qo", last, 0), [("f", last, 0)], quant_out, (last, 0, P)))
         vector_q.append((("qo", last), [], quant_out, (last, P, H)))
 
         for h in range(n + 1):
             if h < n:
                 j, g = steps[h]
-                tensor_q.append((("mm", h), [("q", "z", 0, j), ("q", "z", 1, j)] + [("q", "x", r, s, g) for r in range(2) for s in range(2)], products, (h,)))
+                pairs = [(u, r) for r in range(2) for u in range(2)] if h == 0 else [(u, r) for u in range(2) for r in range(2)]
+                tensor_q += [(("mm", h, u, r), [("q", "z", r, j), ("q", "x", r, 0, g), ("q", "x", r, 1, g)], product, (h, u, r)) for u, r in pairs]
             if h >= 1:
                 tensor_q += [(("t", h - 1, u), [("d", h - 1, u)], turn, (h - 1, u)) for u in range(2)]
 

@@ -17,294 +17,287 @@ ACT = mybir.ActivationFunctionType
 
 P = 128
 PACK = 4
-KP = P * PACK
-W = 512
-H = 256
+GROUP = P * PACK
+UNIT = 512
+STEP = 256
+BLOCK = 2 * STEP
+N_TILES = F // P
 
-XH = [0, 0, 0, 0]
-LO = [0, 2, 8, 9, 4, 6, 10, 11]
-G0 = 0
-ZC = [0, 512, 1024, 2048]
-MC = [0, 1024, 2048]
-HEAD = [0, 1, 2, 3, 8, 9, 4, 5, 6, 10, 7, 11]
-VS = [272, 272, 272, 272, 272, 272, 272, 272, 272, 272, 272, 272, 192, 192, 64, 64, 64, 64, 64, 64, 64, 64, 64, 64]
-GS = [0, 0, 0, 0, 0, 0, 0, 0, 0, 0, 0, 0, 0, 0, 256, 256, 256, 256, 256, 256, 256, 256, 256, 256]
-VP = [11, 12, 13, 14, 15, 16, 17, 18, 19, 20, 21, 22, 23, 24, 24, 24, 24]
-CP = [18, 18, 22, 24, 26, 27, 28, 29, 30, 31, 32, 33, 34, 35, 36, 37, 38, 39, 40, 41, 42, 43, 44, 45, 46, 47, 48, 49, 50, 51, 52, 53]
-LP = [20, 20, 20, 20, 20, 20, 20, 20]
-MP = [10, 13, 18, 19]
-STAGE_BUFS = 4
-BIG_BUFS = 7
-Y_BUFS = 4
-ZQ_BUFS = 5
-FL = 3
-QL = 3
-FU = 0
-YB_BUFS = 3
-GB = 2
-QO_FIRST = 0
+DZ_BOUNDS = (0, 512, 1024, 2048)
+MEMORY_BOUNDS = (0, 1024, 2048)
+
+FIRST_UNITS = 12
+FIRST_SPLIT = UNIT // 2
+LATER_SPLIT = 192
+
+UNITS_BEFORE_STEP_0 = 11
+LAG = 3
 
 
 def tile_replica_weight_grad_g2_kernel(tc, xa, dza, xb, dzb, clip_a, clip_b, memory, out_0, out_1, out_2):
     nc = tc.nc
     xs, dzs = (xa, xb), (dza, dzb)
-    steps = [(j, g) for j in range(8) for g in range(2)]
-    if G0:
-        steps[1], steps[2] = steps[2], steps[1]
-    n = len(steps)
-    last = n - 1
-    first_units = [("x", r, s, g) for r in range(2) for s in range(2) for g in range(2)] + [("z", r, j) for r in range(2) for j in range(2)]
-    first_units = first_units[:8] + [first_units[8], first_units[9], first_units[10], first_units[11]]
-    units = [first_units[i] for i in HEAD] + [("z", r, j) for j in range(2, 8) for r in range(2)]
-    early = [("x", r, s, g) for r in range(2) for s in range(2) for g in range(2)] + [("z", r, s, 0) for r in range(2) for s in range(2)]
-    loads = [early[i] for i in LO]
-    loads += [("z", r, s, c) for c in range(1, len(ZC) - 1) for r in range(2) for s in range(2)]
-    for key, at in zip([("m", g, c) for c in range(len(MC) - 1) for g in range(2)], MP):
-        loads.insert(at, key)
+    steps = [(j, g) for j in range(F // STEP) for g in range(2)]
+    n_steps = len(steps)
+    last = n_steps - 1
 
-    def chunk(cuts, col):
-        return max(c for c in range(len(cuts) - 1) if cuts[c] <= col)
+    units = []
+    for r in range(2):
+        units += [("x", r, s, g) for s in range(2) for g in range(2)] + [("z", r, 0), ("z", r, 1)]
+    last_x = units.index(("x", 1, 1, 1))
+    units[last_x:last_x + 2] = [("z", 1, 0), ("x", 1, 1, 1)]
+    units += [("z", r, j) for j in range(2, F // STEP) for r in range(2)]
+
+    def dz_loads(r, chunk):
+        return [("z", r, s, chunk) for s in range(2)]
+
+    loads = []
+    for r in range(2):
+        loads += [("x", r, 0), ("x", r, 1)] + dz_loads(r, 0)
+    loads += dz_loads(0, 1) + [("m", 0, 0)] + dz_loads(1, 1) + [("m", 1, 0)]
+    loads += dz_loads(0, 2) + dz_loads(1, 2) + [("m", 0, 1), ("m", 1, 1)]
+
+    def chunk_of(bounds, column):
+        return max(chunk for chunk in range(len(bounds) - 1) if bounds[chunk] <= column)
+
+    def loads_of(i):
+        unit = units[i]
+        return [unit[:3]] if unit[0] == "x" else dz_loads(unit[1], chunk_of(DZ_BOUNDS, unit[2] * STEP))
 
     with ExitStack() as ctx:
         keep = ctx.enter_context(tc.tile_pool(name="keep", bufs=1))
-        work = ctx.enter_context(tc.tile_pool(name="work", bufs=3))
+        work = ctx.enter_context(tc.tile_pool(name="work", bufs=1))
         psum = ctx.enter_context(tc.psum_pool(name="psum", bufs=1))
         ctx.enter_context(tc.manual_schedule())
 
-        raw, stage, codes, scales, banks, first, both, turned, ys, ybf, words = {}, {}, {}, {}, {}, {}, {}, {}, {}, {}, {}
+        raw, woven, codes, scales = {}, {}, {}, {}
+        banks, scaled_a, summed, turned = {}, {}, {}, {}
+        y_f32, y_bf16, y_words = {}, {}, {}
 
         def load(key):
             if key[0] == "m":
-                g, c = key[1:]
-                src, tag, bufs = memory[g * KP:(g + 1) * KP, MC[c]:MC[c + 1]], "mem%d" % c, 2
+                g, chunk = key[1:]
+                src = memory[g * GROUP:(g + 1) * GROUP, MEMORY_BOUNDS[chunk]:MEMORY_BOUNDS[chunk + 1]]
+                tag, bufs = "memory%d" % chunk, 2
             elif key[0] == "x":
-                r, s, g = key[1:]
-                if XH[2 * r + s]:
-                    src, tag, bufs = xs[r][s * KP:(s + 1) * KP, g * W:(g + 1) * W], "xh", 2 * sum(XH)
-                else:
-                    src, tag, bufs = xs[r][s * KP:(s + 1) * KP, :], "big", BIG_BUFS
+                r, s = key[1:]
+                src = xs[r][s * GROUP:(s + 1) * GROUP, :]
+                tag, bufs = "wide", 6
             else:
-                r, s, c = key[1:]
-                src = dzs[r][s * KP:(s + 1) * KP, ZC[c]:ZC[c + 1]]
-                tag, bufs = ("big", BIG_BUFS) if src.shape[1] == D else ("z%d" % c, 4)
+                r, s, chunk = key[1:]
+                src = dzs[r][s * GROUP:(s + 1) * GROUP, DZ_BOUNDS[chunk]:DZ_BOUNDS[chunk + 1]]
+                tag, bufs = ("wide", 6) if src.shape[1] == D else ("dz%d" % chunk, 4)
             raw[key] = work.tile([P, PACK, src.shape[1]], BF16, name=tag, tag=tag, bufs=bufs)
             nc.sync.dma_start(out=raw[key][:], in_=src.rearrange("(p t) c -> p t c", t=PACK))
 
-        def copy_on(eng, dst, src):
-            if eng == "V":
+        def copy_on(engine, dst, src):
+            if engine == "vector":
                 nc.vector.tensor_copy(out=dst, in_=src)
-            elif eng == "S":
+            elif engine == "scalar":
                 nc.scalar.copy(out=dst, in_=src)
             else:
                 nc.gpsimd.tensor_scalar(out=dst, in0=src, scalar1=1.0, scalar2=0.0, op0=ALU.mult, op1=ALU.add)
 
-        def weave(eng, dst, src):
-            if eng == "G":
-                copy_on(eng, dst, src.rearrange("p t c -> p c t"))
+        def interleave(engine, dst, src):
+            if engine == "gpsimd":
+                copy_on(engine, dst, src.rearrange("p t c -> p c t"))
             else:
-                copy_on(eng, dst.rearrange("p (c i) t -> p c t i", i=4), src.rearrange("p t (c i) -> p c t i", i=4))
+                copy_on(engine, dst.rearrange("p (c i) t -> p c t i", i=4), src.rearrange("p t (c i) -> p c t i", i=4))
 
-        def unit_loads(i):
-            u = units[i]
-            if u[0] == "x":
-                return [u if XH[2 * u[1] + u[2]] else u[:3] + (0,)]
-            return [("z", u[1], s, chunk(ZC, u[2] * H)) for s in range(2)]
-
-        def weave_unit(i, eng, lo, hi):
-            u = units[i]
-            if i not in stage:
-                stage[i] = work.tile([P, W, PACK], BF16, name="stage", tag="stage%d" % (i % (STAGE_BUFS if i < 12 else GB)), bufs=1, align_bytes=64)
-            if u[0] == "x":
-                if hi > lo:
-                    dst = stage[i][:].rearrange("p (e m) t -> p m t e", e=PACK)
-                    g0 = 0 if XH[2 * u[1] + u[2]] else u[3] * W
-                    src = raw[unit_loads(i)[0]][:, :, g0:g0 + W].rearrange("p t (m e) -> p m t e", e=PACK)
-                    copy_on(eng, dst[:, lo // PACK:hi // PACK, :, :], src[:, lo // PACK:hi // PACK, :, :])
+        def weave(i, engine, lo, hi):
+            unit = units[i]
+            if i not in woven:
+                tag = "woven%d" % (i % (4 if i < FIRST_UNITS - 2 else 2))
+                woven[i] = work.tile([P, UNIT, PACK], BF16, name="woven", tag=tag, bufs=1, align_bytes=64)
+            if unit[0] == "x":
+                g = unit[3]
+                dst = woven[i][:].rearrange("p (e m) t -> p m t e", e=PACK)
+                src = raw[unit[:3]][:, :, g * UNIT:(g + 1) * UNIT].rearrange("p t (m e) -> p m t e", e=PACK)
+                copy_on(engine, dst[:, lo // PACK:hi // PACK, :, :], src[:, lo // PACK:hi // PACK, :, :])
                 return
-            for s, key in enumerate(unit_loads(i)):
-                a, b = max(lo, s * H), min(hi, (s + 1) * H)
+            for s, key in enumerate(loads_of(i)):
+                a, b = max(lo, s * STEP), min(hi, (s + 1) * STEP)
                 if b > a:
-                    off = u[2] * H - ZC[key[3]] - s * H
-                    weave(eng, stage[i][:, a:b, :], raw[key][:, :, a + off:b + off])
+                    shift = unit[2] * STEP - DZ_BOUNDS[key[3]] - s * STEP
+                    interleave(engine, woven[i][:, a:b, :], raw[key][:, :, a + shift:b + shift])
 
-        def quant_in(i):
-            u = units[i]
-            tag, bufs = ("xq", 8) if u[0] == "x" else ("zq", ZQ_BUFS)
-            codes[u] = work.tile([P, W], U32, name=tag + "c", tag=tag + "c", bufs=bufs, align_bytes=64)
-            scales[u] = work.tile([P, W], U8, name=tag + "s", tag=tag + "s", bufs=bufs, align_bytes=64)
-            nc.vector.quantize_mx(out=codes[u][:].bitcast(FP8X4), scales=scales[u][:], in_=stage[i][:].rearrange("p c t -> p (c t)"))
+        def quantize_unit(i):
+            unit = units[i]
+            tag, bufs = ("x", 8) if unit[0] == "x" else ("z", 5)
+            codes[unit] = work.tile([P, UNIT], U32, name="codes", tag=tag + "codes", bufs=bufs, align_bytes=64)
+            scales[unit] = work.tile([P, UNIT], U8, name="scales", tag=tag + "scales", bufs=bufs, align_bytes=64)
+            nc.vector.quantize_mx(out=codes[unit][:].bitcast(FP8X4), scales=scales[unit][:],
+                                  in_=woven[i][:].rearrange("p c t -> p (c t)"))
 
         def product(h, u, r):
             j, g = steps[h]
-            banks[h, u, r] = psum.tile([P, W], F32, name="ab"[r], tag="ab"[r], bufs=3)
+            banks[h, u, r] = psum.tile([P, UNIT], F32, name="product", tag="product%d" % r, bufs=3)
             for s in range(2):
-                cols = slice(s * H + u * P, s * H + (u + 1) * P)
+                cols = slice(s * STEP + u * P, s * STEP + (u + 1) * P)
                 nc.tensor.matmul_mx(
                     out=banks[h, u, r][:],
                     lhsT=codes["z", r, j][:, cols].bitcast(FP8X4), lhsT_scale=scales["z", r, j][:, cols],
                     rhs=codes["x", r, s, g][:].bitcast(FP8X4), rhs_scale=scales["x", r, s, g][:],
                     start=(s == 0), stop=(s == 1))
 
-        def clip_first(h, u):
-            c = 2 * steps[h][0] + u
-            first[h, u] = work.tile([P, W], F32, name="first", tag="first", bufs=4)
-            nc.scalar.activation(out=first[h, u][:], in_=banks[h, u, 0][:], func=ACT.Copy, scale=clips[:, c:c + 1])
+        def clip_replica_a(h, u):
+            col = 2 * steps[h][0] + u
+            scaled_a[h, u] = work.tile([P, UNIT], F32, name="scaled_a", tag="scaled_a", bufs=4)
+            nc.scalar.activation(out=scaled_a[h, u][:], in_=banks[h, u, 0][:], func=ACT.Copy, scale=clips[:, col:col + 1])
 
-        def clip_second(h, u):
-            c = 16 + 2 * steps[h][0] + u
-            both[h, u] = work.tile([P, W], F32, name="both", tag="both", bufs=4)
-            nc.vector.scalar_tensor_tensor(out=both[h, u][:], in0=banks[h, u, 1][:],
-                                           scalar=clips[:, c:c + 1], in1=first[h, u][:], op0=ALU.mult, op1=ALU.add)
+        def clip_replica_b_and_add(h, u):
+            col = N_TILES + 2 * steps[h][0] + u
+            summed[h, u] = work.tile([P, UNIT], F32, name="summed", tag="summed", bufs=4)
+            nc.vector.scalar_tensor_tensor(out=summed[h, u][:], in0=banks[h, u, 1][:], scalar=clips[:, col:col + 1],
+                                           in1=scaled_a[h, u][:], op0=ALU.mult, op1=ALU.add)
 
         def turn(h, u):
             turned[h, u] = psum.tile([P, PACK, P], F32, name="turned", tag="turned", bufs=2)
             for t in range(PACK):
-                nc.tensor.transpose(out=turned[h, u][:, t, :], in_=both[h, u][:, t * P:(t + 1) * P], identity=ident[:])
+                nc.tensor.transpose(out=turned[h, u][:, t, :], in_=summed[h, u][:, t * P:(t + 1) * P], identity=ident[:])
 
         def add_memory(h, u):
             j, g = steps[h]
-            if u == 0:
-                if j % 2 == 0:
-                    ys[j // 2, g] = work.tile([P, PACK, W], F32, name="y", tag="y", bufs=Y_BUFS)
-            c = chunk(MC, j * H)
-            c0 = j * H + u * P - MC[c]
-            y0 = (j % 2) * H + u * P
-            nc.vector.tensor_tensor(out=ys[j // 2, g][:, :, y0:y0 + P], in0=turned[h, u][:],
-                                    in1=raw["m", g, c][:, :, c0:c0 + P], op=ALU.add)
+            if u == 0 and j % 2 == 0:
+                y_f32[j // 2, g] = work.tile([P, PACK, BLOCK], F32, name="y_f32", tag="y_f32", bufs=4)
+            chunk = chunk_of(MEMORY_BOUNDS, j * STEP)
+            m0 = j * STEP + u * P - MEMORY_BOUNDS[chunk]
+            y0 = (j % 2) * STEP + u * P
+            nc.vector.tensor_tensor(out=y_f32[j // 2, g][:, :, y0:y0 + P], in0=turned[h, u][:],
+                                    in1=raw["m", g, chunk][:, :, m0:m0 + P], op=ALU.add)
 
-        def round_y(h, lo, hi, eng):
+        def round_y(h, lo, hi, engine):
             j, g = steps[h]
-            if h not in ybf:
-                ybf[h] = work.tile([P, H, PACK], BF16, name="ybf", tag="ybf", bufs=YB_BUFS, align_bytes=64)
-            y0 = (j % 2) * H
-            weave(eng, ybf[h][:, lo:hi, :], ys[j // 2, g][:, :, y0 + lo:y0 + hi])
+            if lo == 0:
+                y_bf16[h] = work.tile([P, STEP, PACK], BF16, name="y_bf16", tag="y_bf16", bufs=3, align_bytes=64)
+            y0 = (j % 2) * STEP
+            interleave(engine, y_bf16[h][:, lo:hi, :], y_f32[j // 2, g][:, :, y0 + lo:y0 + hi])
 
-        def quant_out(h, lo, hi):
+        def quantize_y(h, lo, hi):
             j, g = steps[h]
             if lo == 0 and j % 2 == 0:
-                words[j // 2, g] = work.tile([P, W], U32, name="words", tag="words", bufs=4, align_bytes=64)
-            y0 = (j % 2) * H
-            nc.vector.quantize_mx(out=words[j // 2, g][:, y0 + lo:y0 + hi].bitcast(FP8X4), scales=out_scales[:, g, j * H + lo:j * H + hi],
-                                  in_=ybf[h][:, lo:hi, :].rearrange("p c t -> p (c t)"))
+                y_words[j // 2, g] = work.tile([P, BLOCK], U32, name="y_words", tag="y_words", bufs=4, align_bytes=64)
+            y0 = (j % 2) * STEP
+            nc.vector.quantize_mx(out=y_words[j // 2, g][:, y0 + lo:y0 + hi].bitcast(FP8X4),
+                                  scales=y_scales[:, g, j * STEP + lo:j * STEP + hi],
+                                  in_=y_bf16[h][:, lo:hi, :].rearrange("p c t -> p (c t)"))
 
         def store_y(q, g, lo, hi):
-            nc.sync.dma_start(out=out_0[g * KP:(g + 1) * KP, q * W + lo:q * W + hi].rearrange("(p t) c -> p t c", t=PACK), in_=ys[q, g][:, :, lo:hi])
+            dst = out_0[g * GROUP:(g + 1) * GROUP, q * BLOCK + lo:q * BLOCK + hi]
+            nc.sync.dma_start(out=dst.rearrange("(p t) c -> p t c", t=PACK), in_=y_f32[q, g][:, :, lo:hi])
 
         def store_words(q, g, lo, hi):
-            nc.sync.dma_start(out=out_1[g, :, q * W + lo:q * W + hi, :].rearrange("p m t -> p (m t)").bitcast(I32), in_=words[q, g][:, lo:hi].bitcast(I32))
+            dst = out_1[g, :, q * BLOCK + lo:q * BLOCK + hi, :].rearrange("p m t -> p (m t)")
+            nc.sync.dma_start(out=dst.bitcast(I32), in_=y_words[q, g][:, lo:hi].bitcast(I32))
 
-        def store_scales(lo, hi, quads, eng):
-            for q in quads:
-                eng.dma_start(out=out_2[:, 4 * q:4 * q + 4, lo:hi].rearrange("g r m -> r g m").bitcast(I32),
-                              in_=out_scales[32 * q:32 * q + 4, :, lo:hi].bitcast(I32))
+        def store_scales(lo, hi, quadrants, engine):
+            for quad in quadrants:
+                dst = out_2[:, 4 * quad:4 * quad + 4, lo:hi].rearrange("g r m -> r g m")
+                engine.dma_start(out=dst.bitcast(I32), in_=y_scales[32 * quad:32 * quad + 4, :, lo:hi].bitcast(I32))
 
-        out_scales = keep.tile([P, 2, F], U8, name="out_scales", align_bytes=64)
+        y_scales = keep.tile([P, 2, F], U8, name="y_scales", align_bytes=64)
         ident = keep.tile([P, P], F32, name="ident")
-        clip_rows = keep.tile([32, P], BF16, name="clip_rows")
-        clip_wide = keep.tile([P, P], F32, name="clip_wide")
-        clips = keep.tile([P, 32], F32, name="clips")
-        nc.scalar.dma_start(out=clip_rows[0:16, :], in_=clip_a.rearrange("(c p) -> c p", p=P))
-        nc.scalar.dma_start(out=clip_rows[16:32, :], in_=clip_b.rearrange("(c p) -> c p", p=P))
+        clip_rows = keep.tile([2 * N_TILES, P], BF16, name="clip_rows")
+        clip_square = keep.tile([P, P], F32, name="clip_square")
+        clips = keep.tile([P, 2 * N_TILES], F32, name="clips")
+        nc.scalar.dma_start(out=clip_rows[0:N_TILES, :], in_=clip_a.rearrange("(c p) -> c p", p=P))
+        nc.scalar.dma_start(out=clip_rows[N_TILES:2 * N_TILES, :], in_=clip_b.rearrange("(c p) -> c p", p=P))
         make_identity(nc, ident[:])
-        nc.scalar.activation(out=clip_wide[:], in_=ident[:], func=ACT.Copy, scale=0.0)
-        clip_psum = psum.tile([P, PACK, P], F32, name="turned", tag="turned", bufs=2)
+        nc.scalar.activation(out=clip_square[:], in_=ident[:], func=ACT.Copy, scale=0.0)
+        clip_bank = psum.tile([P, PACK, P], F32, name="turned", tag="turned", bufs=2)
 
-        def widen_clips():
-            nc.scalar.copy(out=clip_wide[0:32, :], in_=clip_rows[:])
-            nc.tensor.transpose(out=clip_psum[:, 0, :], in_=clip_wide[:], identity=ident[:])
+        def turn_clips():
+            nc.scalar.copy(out=clip_square[0:2 * N_TILES, :], in_=clip_rows[:])
+            nc.tensor.transpose(out=clip_bank[:, 0, :], in_=clip_square[:], identity=ident[:])
 
-        sync_q, scalar_q, vector_q, gpsimd_q, tensor_q = [], [], [], [], []
-        done = 0
-        stores = []
-        for k in range(1, n + QL + 1):
-            for h, kind, call in ((k - QL, "qo", store_words), (k - 1, "e", store_y)):
-                if 0 <= h < n and (steps[h][0] % 2 == 1 or steps[h][0] == 6):
+        def fetch_clips():
+            nc.scalar.copy(out=clips[:], in_=clip_bank[:, 0, 0:2 * N_TILES])
+
+
+        sync_order = [(key, [], load, (key,)) for key in loads]
+        last_block = F // BLOCK - 1
+        for k in range(1, n_steps + LAG):
+            for h, kind in ((k - LAG, "words"), (k - 1, "y")):
+                if 0 <= h < n_steps and (steps[h][0] % 2 == 1 or steps[h][0] // 2 == last_block):
                     j, g = steps[h]
-                    lo, hi = (0, W) if j < 6 else ((j - 6) * H, (j - 5) * H)
-                    stores.append(((kind + "s", h), [("qo", h) if kind == "qo" else ("e", h, 1)], call, (j // 2, g, lo, hi)))
-            if k - QL == last - 4:
-                stores.append((("ss", 0), [], store_scales, (0, F - W, range(4), nc.sync)))
-        stores.append((("ss", 1), [("qo", last)], store_scales, (F - W, F, range(2), nc.sync)))
-        for b, store in enumerate(stores):
-            at = min(LP[b], len(loads)) if b < len(LP) else len(loads)
-            sync_q += [(key, [], load, (key,)) for key in loads[done:at]]
-            done = max(done, at)
-            sync_q.append(store)
+                    lo, hi = (0, BLOCK) if j // 2 < last_block else ((j % 2) * STEP, (j % 2 + 1) * STEP)
+                    if kind == "words":
+                        sync_order.append((("store words", h), [("quantize y", h)], store_words, (j // 2, g, lo, hi)))
+                    elif h < last:
+                        sync_order.append((("store y", h), [("add", h, 1)], store_y, (j // 2, g, lo, hi)))
+                    else:
+                        sync_order += [(("store y", h, u), [("add", h, u)], store_y, (j // 2, g, lo + u * P, lo + (u + 1) * P))
+                                       for u in range(2)]
+            if k - LAG == 4 * last_block - 1:
+                sync_order.append(("early scales", [], store_scales, (0, F - BLOCK, range(4), nc.sync)))
+        sync_order.append(("last scales 0", [], store_scales, (F - BLOCK, F, range(2), nc.sync)))
 
-        helped = {}
-        for k in range(1, n + 1):
-            i = max(VP[:k + 1]) - 1 + GB
-            if i < len(units) and i not in helped.values() and GS[i] > 0:
-                helped[k] = i
-        share = [W - (min(GS[i], W - VS[i]) if i in helped.values() else 0) for i in range(len(units))]
-
-        pieces = []
-        for i in range(len(units)):
-            mid = H if units[i][0] == "z" and VS[i] < H < share[i] else (VS[i] + share[i]) // 32 * 16
-            pieces += [(("ws", i, 0), unit_loads(i), weave_unit, (i, "S", VS[i], mid)),
-                       (("ws", i, 1), unit_loads(i), weave_unit, (i, "S", mid, share[i]))]
+        scalar_order = []
         done = 0
-        for c in range(2 * n):
-            h, u = divmod(c, 2)
-            at = min(CP[c], len(pieces))
-            scalar_q += pieces[done:at]
-            done = max(done, at)
-            if h >= FL and u == FU:
-                scalar_q.append((("f", h - FL), [("e", h - FL, 1)], round_y, (h - FL, 0, H, "S")))
-            scalar_q.append((("c", h, u), [("mm", h, u, 0), "clips"], clip_first, (h, u)))
-        scalar_q += pieces[done:]
-        scalar_q += [(("f", h), [("e", h, 1)], round_y, (h, 0, H, "S")) for h in range(n - FL, last)]
-        scalar_q.append((("f", last, 0), [("e", last, 0)], round_y, (last, 0, P, "S")))
-        scalar_q.append((("ss", 2), [("qo", last)], store_scales, (F - W, F, range(2, 4), nc.scalar)))
-        scalar_q.insert(4, ("widen", [], widen_clips, ()))
-        scalar_q.insert(7, ("clips", [], lambda: nc.scalar.copy(out=clips[:], in_=clip_psum[:, 0, 0:32]), ()))
+        for h in range(n_steps):
+            for u in range(2):
+                ahead = (units.index(("z", 1, 0)), FIRST_UNITS)[h] if h < 2 else min(UNITS_BEFORE_STEP_0 + h + u, len(units))
+                for i in range(done, ahead):
+                    lo, hi = (FIRST_SPLIT, UNIT) if i < FIRST_UNITS else (0, LATER_SPLIT)
+                    scalar_order.append((("weave scalar", i), loads_of(i), weave, (i, "scalar", lo, hi)))
+                done = ahead
+                if u == 0 and h >= LAG:
+                    scalar_order.append((("round", h - LAG), [("add", h - LAG, 1)], round_y, (h - LAG, 0, STEP, "scalar")))
+                scalar_order.append((("clip a", h, u), [("product", h, u, 0), "clips"], clip_replica_a, (h, u)))
+        scalar_order += [(("round", h), [("add", h, 1)], round_y, (h, 0, STEP, "scalar")) for h in range(n_steps - LAG, last)]
+        scalar_order.append((("round", last, 0), [("add", last, 0)], round_y, (last, 0, P, "scalar")))
+        scalar_order.append(("last scales 1", [("quantize y", last)], store_scales, (F - BLOCK, F, range(2, 4), nc.scalar)))
+        scalar_order.insert(2, ("turn clips", [], turn_clips, ()))
+        scalar_order.insert(4, ("clips", [], fetch_clips, ()))
 
-        prep = [[(("wv", 0), unit_loads(0), weave_unit, (0, "V", 0, VS[0]))]] + [[] for i in units[1:]]
-        for i in range(len(units)):
-            if i + 1 < len(units):
-                prep[i].append((("wv", i + 1), unit_loads(i + 1), weave_unit, (i + 1, "V", 0, VS[i + 1])))
-            prep[i].append((("q",) + units[i], [("ws", i, 1)] + ([("wg", i)] if i in helped.values() else []), quant_in, (i,)))
+        vector_order = [(("weave vector", 0), loads_of(0), weave, (0, "vector", 0, FIRST_SPLIT))]
+        gpsimd_order = []
         done = 0
-        for k in range(n + 1):
-            part = []
-            for i in range(done, VP[k]):
-                part += prep[i]
-            done = max(done, VP[k])
-            if k >= QL:
-                part.insert(max(len(part) - QO_FIRST, 0), (("qo", k - QL), [("f", k - QL)], quant_out, (k - QL, 0, H)))
-            vector_q += part
-            if k in helped:
-                i = helped[k]
-                gpsimd_q.append((("wg", i), unit_loads(i) + [("q",) + units[i - GB]], weave_unit, (i, "G", share[i], W)))
+        for k in range(n_steps + 1):
+            due = min(UNITS_BEFORE_STEP_0 + k, len(units))
+            for i in range(done, due):
+                if i + 1 < FIRST_UNITS:
+                    vector_order.append((("weave vector", i + 1), loads_of(i + 1), weave, (i + 1, "vector", 0, FIRST_SPLIT)))
+                shares = [("weave scalar", i)] + ([("weave gpsimd", i)] if i >= FIRST_UNITS else [])
+                vector_order.append((("quantize",) + units[i], shares, quantize_unit, (i,)))
+            done = due
+            if k >= LAG:
+                vector_order.append((("quantize y", k - LAG), [("round", k - LAG)], quantize_y, (k - LAG, 0, STEP)))
+            if due + 1 < len(units):
+                needs = loads_of(due + 1) + [("quantize",) + units[due - 1]]
+                gpsimd_order.append((("weave gpsimd", due + 1), needs, weave, (due + 1, "gpsimd", LATER_SPLIT, UNIT)))
             if k >= 1:
                 j, g = steps[k - 1]
-                for u in range(2):
-                    vector_q.append((("e", k - 1, u), [("t", k - 1, u), ("m", g, chunk(MC, j * H))], add_memory, (k - 1, u)))
-            if k < n:
-                vector_q += [(("d", k, u), [("c", k, u), ("mm", k, u, 1)], clip_second, (k, u)) for u in range(2)]
-        vector_q += [(("qo", h), [("f", h)], quant_out, (h, 0, H)) for h in range(n + 1 - QL, last)]
-        vector_q.append((("f", last, 1), [], round_y, (last, P, H, "V")))
-        vector_q.append((("qo", last, 0), [("f", last, 0)], quant_out, (last, 0, P)))
-        vector_q.append((("qo", last), [], quant_out, (last, P, H)))
+                memory_load = ("m", g, chunk_of(MEMORY_BOUNDS, j * STEP))
+                vector_order += [(("add", k - 1, u), [("turn", k - 1, u), memory_load], add_memory, (k - 1, u)) for u in range(2)]
+            if k < n_steps:
+                vector_order += [(("sum", k, u), [("clip a", k, u), ("product", k, u, 1)], clip_replica_b_and_add, (k, u))
+                                 for u in range(2)]
+        vector_order += [(("quantize y", h), [("round", h)], quantize_y, (h, 0, STEP)) for h in range(n_steps + 1 - LAG, last)]
+        vector_order.append((("round", last, 1), [("round", last, 0)], round_y, (last, P, STEP, "vector")))
+        vector_order.append((("quantize y", last, 0), [], quantize_y, (last, 0, P)))
+        vector_order.append((("quantize y", last), [], quantize_y, (last, P, STEP)))
 
-        for h in range(n + 1):
-            if h < n:
+        tensor_order = []
+        for h in range(n_steps + 1):
+            if h < n_steps:
                 j, g = steps[h]
                 pairs = [(u, r) for r in range(2) for u in range(2)] if h == 0 else [(u, r) for u in range(2) for r in range(2)]
-                tensor_q += [(("mm", h, u, r), [("q", "z", r, j), ("q", "x", r, 0, g), ("q", "x", r, 1, g)], product, (h, u, r)) for u, r in pairs]
+                for u, r in pairs:
+                    needs = [("quantize", "z", r, j), ("quantize", "x", r, 0, g), ("quantize", "x", r, 1, g)]
+                    tensor_order.append((("product", h, u, r), needs, product, (h, u, r)))
             if h >= 1:
-                tensor_q += [(("t", h - 1, u), [("d", h - 1, u)], turn, (h - 1, u)) for u in range(2)]
+                tensor_order += [(("turn", h - 1, u), [("sum", h - 1, u)], turn, (h - 1, u)) for u in range(2)]
 
+        orders = [sync_order, scalar_order, vector_order, gpsimd_order, tensor_order]
+        heads = [0] * len(orders)
         written = set()
-        queues = [sync_q, scalar_q, vector_q, gpsimd_q, tensor_q]
-        heads = [0] * len(queues)
-        while any(heads[e] < len(q) for e, q in enumerate(queues)):
-            moved = False
-            for e, q in enumerate(queues):
-                while heads[e] < len(q) and all(k in written for k in q[heads[e]][1]):
-                    name, needs, call, args = q[heads[e]]
+        while any(heads[e] < len(order) for e, order in enumerate(orders)):
+            before = sum(heads)
+            for e, order in enumerate(orders):
+                while heads[e] < len(order) and all(name in written for name in order[heads[e]][1]):
+                    name, needs, call, args = order[heads[e]]
                     call(*args)
                     written.add(name)
                     heads[e] += 1
-                    moved = True
-            assert moved
+            assert sum(heads) > before

from contextlib import ExitStack

import concourse.mybir as mybir
from concourse.masks import make_identity

T, D, F = 1024, 1024, 2048
FLOPS = 2 * 2 * T * D * F

F32 = mybir.dt.float32
BF16 = mybir.dt.bfloat16
U32 = mybir.dt.uint32
I32 = mybir.dt.int32
U8 = mybir.dt.uint8
FP8X4 = mybir.dt.float8_e4m3fn_x4
ALU = mybir.AluOpType
ACT = mybir.ActivationFunctionType

P = 128
PACK = 4
GROUP = P * PACK
UNIT = 512
STEP = 256
BLOCK = 2 * STEP
N_TILES = F // P

DZ_BOUNDS = (0, 512, 1024, 2048)
MEMORY_BOUNDS = (0, 1024, 2048)

FIRST_UNITS = 12
FIRST_SPLIT = UNIT // 2
LATER_SPLIT = 192

UNITS_BEFORE_STEP_0 = 11
LAG = 3


def tile_replica_weight_grad_g2_kernel(tc, xa, dza, xb, dzb, clip_a, clip_b, memory, out_0, out_1, out_2):
    nc = tc.nc
    xs, dzs = (xa, xb), (dza, dzb)
    steps = [(j, g) for j in range(F // STEP) for g in range(2)]
    n_steps = len(steps)
    last = n_steps - 1

    units = []
    for r in range(2):
        units += [("x", r, s, g) for s in range(2) for g in range(2)] + [("z", r, 0), ("z", r, 1)]
    last_x = units.index(("x", 1, 1, 1))
    units[last_x:last_x + 2] = [("z", 1, 0), ("x", 1, 1, 1)]
    units += [("z", r, j) for j in range(2, F // STEP) for r in range(2)]

    def dz_loads(r, chunk):
        return [("z", r, s, chunk) for s in range(2)]

    loads = []
    for r in range(2):
        loads += [("x", r, 0), ("x", r, 1)] + dz_loads(r, 0)
    loads += dz_loads(0, 1) + [("m", 0, 0)] + dz_loads(1, 1) + [("m", 1, 0)]
    loads += dz_loads(0, 2) + dz_loads(1, 2) + [("m", 0, 1), ("m", 1, 1)]

    def chunk_of(bounds, column):
        return max(chunk for chunk in range(len(bounds) - 1) if bounds[chunk] <= column)

    def loads_of(i):
        unit = units[i]
        return [unit[:3]] if unit[0] == "x" else dz_loads(unit[1], chunk_of(DZ_BOUNDS, unit[2] * STEP))

    with ExitStack() as ctx:
        keep = ctx.enter_context(tc.tile_pool(name="keep", bufs=1))
        work = ctx.enter_context(tc.tile_pool(name="work", bufs=1))
        psum = ctx.enter_context(tc.psum_pool(name="psum", bufs=1))
        ctx.enter_context(tc.manual_schedule())

        raw, woven, codes, scales = {}, {}, {}, {}
        banks, scaled_a, summed, turned = {}, {}, {}, {}
        y_f32, y_bf16, y_words = {}, {}, {}

        def load(key):
            if key[0] == "m":
                g, chunk = key[1:]
                src = memory[g * GROUP:(g + 1) * GROUP, MEMORY_BOUNDS[chunk]:MEMORY_BOUNDS[chunk + 1]]
                tag, bufs = "memory%d" % chunk, 2
            elif key[0] == "x":
                r, s = key[1:]
                src = xs[r][s * GROUP:(s + 1) * GROUP, :]
                tag, bufs = "wide", 6
            else:
                r, s, chunk = key[1:]
                src = dzs[r][s * GROUP:(s + 1) * GROUP, DZ_BOUNDS[chunk]:DZ_BOUNDS[chunk + 1]]
                tag, bufs = ("wide", 6) if src.shape[1] == D else ("dz%d" % chunk, 4)
            raw[key] = work.tile([P, PACK, src.shape[1]], BF16, name=tag, tag=tag, bufs=bufs)
            nc.sync.dma_start(out=raw[key][:], in_=src.rearrange("(p t) c -> p t c", t=PACK))

        def copy_on(engine, dst, src):
            if engine == "vector":
                nc.vector.tensor_copy(out=dst, in_=src)
            elif engine == "scalar":
                nc.scalar.copy(out=dst, in_=src)
            else:
                nc.gpsimd.tensor_scalar(out=dst, in0=src, scalar1=1.0, scalar2=0.0, op0=ALU.mult, op1=ALU.add)

        def interleave(engine, dst, src):
            if engine == "gpsimd":
                copy_on(engine, dst, src.rearrange("p t c -> p c t"))
            else:
                copy_on(engine, dst.rearrange("p (c i) t -> p c t i", i=4), src.rearrange("p t (c i) -> p c t i", i=4))

        def weave(i, engine, lo, hi):
            unit = units[i]
            if i not in woven:
                tag = "woven%d" % (i % (4 if i < FIRST_UNITS - 2 else 2))
                woven[i] = work.tile([P, UNIT, PACK], BF16, name="woven", tag=tag, bufs=1, align_bytes=64)
            if unit[0] == "x":
                g = unit[3]
                dst = woven[i][:].rearrange("p (e m) t -> p m t e", e=PACK)
                src = raw[unit[:3]][:, :, g * UNIT:(g + 1) * UNIT].rearrange("p t (m e) -> p m t e", e=PACK)
                copy_on(engine, dst[:, lo // PACK:hi // PACK, :, :], src[:, lo // PACK:hi // PACK, :, :])
                return
            for s, key in enumerate(loads_of(i)):
                a, b = max(lo, s * STEP), min(hi, (s + 1) * STEP)
                if b > a:
                    shift = unit[2] * STEP - DZ_BOUNDS[key[3]] - s * STEP
                    interleave(engine, woven[i][:, a:b, :], raw[key][:, :, a + shift:b + shift])

        def quantize_unit(i):
            unit = units[i]
            tag, bufs = ("x", 8) if unit[0] == "x" else ("z", 5)
            codes[unit] = work.tile([P, UNIT], U32, name="codes", tag=tag + "codes", bufs=bufs, align_bytes=64)
            scales[unit] = work.tile([P, UNIT], U8, name="scales", tag=tag + "scales", bufs=bufs, align_bytes=64)
            nc.vector.quantize_mx(out=codes[unit][:].bitcast(FP8X4), scales=scales[unit][:],
                                  in_=woven[i][:].rearrange("p c t -> p (c t)"))

        def product(h, u, r):
            j, g = steps[h]
            banks[h, u, r] = psum.tile([P, UNIT], F32, name="product", tag="product%d" % r, bufs=3)
            for s in range(2):
                cols = slice(s * STEP + u * P, s * STEP + (u + 1) * P)
                nc.tensor.matmul_mx(
                    out=banks[h, u, r][:],
                    lhsT=codes["z", r, j][:, cols].bitcast(FP8X4), lhsT_scale=scales["z", r, j][:, cols],
                    rhs=codes["x", r, s, g][:].bitcast(FP8X4), rhs_scale=scales["x", r, s, g][:],
                    start=(s == 0), stop=(s == 1))

        def clip_replica_a(h, u):
            col = 2 * steps[h][0] + u
            scaled_a[h, u] = work.tile([P, UNIT], F32, name="scaled_a", tag="scaled_a", bufs=4)
            nc.scalar.activation(out=scaled_a[h, u][:], in_=banks[h, u, 0][:], func=ACT.Copy, scale=clips[:, col:col + 1])

        def clip_replica_b_and_add(h, u):
            col = N_TILES + 2 * steps[h][0] + u
            summed[h, u] = work.tile([P, UNIT], F32, name="summed", tag="summed", bufs=4)
            nc.vector.scalar_tensor_tensor(out=summed[h, u][:], in0=banks[h, u, 1][:], scalar=clips[:, col:col + 1],
                                           in1=scaled_a[h, u][:], op0=ALU.mult, op1=ALU.add)

        def turn(h, u):
            turned[h, u] = psum.tile([P, PACK, P], F32, name="turned", tag="turned", bufs=2)
            for t in range(PACK):
                nc.tensor.transpose(out=turned[h, u][:, t, :], in_=summed[h, u][:, t * P:(t + 1) * P], identity=ident[:])

        def add_memory(h, u):
            j, g = steps[h]
            if u == 0 and j % 2 == 0:
                y_f32[j // 2, g] = work.tile([P, PACK, BLOCK], F32, name="y_f32", tag="y_f32", bufs=4)
            chunk = chunk_of(MEMORY_BOUNDS, j * STEP)
            m0 = j * STEP + u * P - MEMORY_BOUNDS[chunk]
            y0 = (j % 2) * STEP + u * P
            nc.vector.tensor_tensor(out=y_f32[j // 2, g][:, :, y0:y0 + P], in0=turned[h, u][:],
                                    in1=raw["m", g, chunk][:, :, m0:m0 + P], op=ALU.add)

        def round_y(h, lo, hi, engine):
            j, g = steps[h]
            if lo == 0:
                y_bf16[h] = work.tile([P, STEP, PACK], BF16, name="y_bf16", tag="y_bf16", bufs=3, align_bytes=64)
            y0 = (j % 2) * STEP
            interleave(engine, y_bf16[h][:, lo:hi, :], y_f32[j // 2, g][:, :, y0 + lo:y0 + hi])

        def quantize_y(h, lo, hi):
            j, g = steps[h]
            if lo == 0 and j % 2 == 0:
                y_words[j // 2, g] = work.tile([P, BLOCK], U32, name="y_words", tag="y_words", bufs=4, align_bytes=64)
            y0 = (j % 2) * STEP
            nc.vector.quantize_mx(out=y_words[j // 2, g][:, y0 + lo:y0 + hi].bitcast(FP8X4),
                                  scales=y_scales[:, g, j * STEP + lo:j * STEP + hi],
                                  in_=y_bf16[h][:, lo:hi, :].rearrange("p c t -> p (c t)"))

        def store_y(q, g, lo, hi):
            dst = out_0[g * GROUP:(g + 1) * GROUP, q * BLOCK + lo:q * BLOCK + hi]
            nc.sync.dma_start(out=dst.rearrange("(p t) c -> p t c", t=PACK), in_=y_f32[q, g][:, :, lo:hi])

        def store_words(q, g, lo, hi):
            dst = out_1[g, :, q * BLOCK + lo:q * BLOCK + hi, :].rearrange("p m t -> p (m t)")
            nc.sync.dma_start(out=dst.bitcast(I32), in_=y_words[q, g][:, lo:hi].bitcast(I32))

        def store_scales(lo, hi, quadrants, engine):
            for quad in quadrants:
                dst = out_2[:, 4 * quad:4 * quad + 4, lo:hi].rearrange("g r m -> r g m")
                engine.dma_start(out=dst.bitcast(I32), in_=y_scales[32 * quad:32 * quad + 4, :, lo:hi].bitcast(I32))

        y_scales = keep.tile([P, 2, F], U8, name="y_scales", align_bytes=64)
        ident = keep.tile([P, P], F32, name="ident")
        clip_rows = keep.tile([2 * N_TILES, P], BF16, name="clip_rows")
        clip_square = keep.tile([P, P], F32, name="clip_square")
        clips = keep.tile([P, 2 * N_TILES], F32, name="clips")
        nc.scalar.dma_start(out=clip_rows[0:N_TILES, :], in_=clip_a.rearrange("(c p) -> c p", p=P))
        nc.scalar.dma_start(out=clip_rows[N_TILES:2 * N_TILES, :], in_=clip_b.rearrange("(c p) -> c p", p=P))
        make_identity(nc, ident[:])
        nc.scalar.activation(out=clip_square[:], in_=ident[:], func=ACT.Copy, scale=0.0)
        clip_bank = psum.tile([P, PACK, P], F32, name="turned", tag="turned", bufs=2)

        def turn_clips():
            nc.scalar.copy(out=clip_square[0:2 * N_TILES, :], in_=clip_rows[:])
            nc.tensor.transpose(out=clip_bank[:, 0, :], in_=clip_square[:], identity=ident[:])

        def fetch_clips():
            nc.scalar.copy(out=clips[:], in_=clip_bank[:, 0, 0:2 * N_TILES])


        sync_order = [(key, [], load, (key,)) for key in loads]
        last_block = F // BLOCK - 1
        for k in range(1, n_steps + LAG):
            for h, kind in ((k - LAG, "words"), (k - 1, "y")):
                if 0 <= h < n_steps and (steps[h][0] % 2 == 1 or steps[h][0] // 2 == last_block):
                    j, g = steps[h]
                    lo, hi = (0, BLOCK) if j // 2 < last_block else ((j % 2) * STEP, (j % 2 + 1) * STEP)
                    if kind == "words":
                        sync_order.append((("store words", h), [("quantize y", h)], store_words, (j // 2, g, lo, hi)))
                    elif h < last:
                        sync_order.append((("store y", h), [("add", h, 1)], store_y, (j // 2, g, lo, hi)))
                    else:
                        sync_order += [(("store y", h, u), [("add", h, u)], store_y, (j // 2, g, lo + u * P, lo + (u + 1) * P))
                                       for u in range(2)]
            if k - LAG == 4 * last_block - 1:
                sync_order.append(("early scales", [], store_scales, (0, F - BLOCK, range(4), nc.sync)))
        sync_order.append(("last scales 0", [], store_scales, (F - BLOCK, F, range(2), nc.sync)))

        scalar_order = []
        done = 0
        for h in range(n_steps):
            for u in range(2):
                ahead = (units.index(("z", 1, 0)), FIRST_UNITS)[h] if h < 2 else min(UNITS_BEFORE_STEP_0 + h + u, len(units))
                for i in range(done, ahead):
                    lo, hi = (FIRST_SPLIT, UNIT) if i < FIRST_UNITS else (0, LATER_SPLIT)
                    scalar_order.append((("weave scalar", i), loads_of(i), weave, (i, "scalar", lo, hi)))
                done = ahead
                if u == 0 and h >= LAG:
                    scalar_order.append((("round", h - LAG), [("add", h - LAG, 1)], round_y, (h - LAG, 0, STEP, "scalar")))
                scalar_order.append((("clip a", h, u), [("product", h, u, 0), "clips"], clip_replica_a, (h, u)))
        scalar_order += [(("round", h), [("add", h, 1)], round_y, (h, 0, STEP, "scalar")) for h in range(n_steps - LAG, last)]
        scalar_order.append((("round", last, 0), [("add", last, 0)], round_y, (last, 0, P, "scalar")))
        scalar_order.append(("last scales 1", [("quantize y", last)], store_scales, (F - BLOCK, F, range(2, 4), nc.scalar)))
        scalar_order.insert(2, ("turn clips", [], turn_clips, ()))
        scalar_order.insert(4, ("clips", [], fetch_clips, ()))

        vector_order = [(("weave vector", 0), loads_of(0), weave, (0, "vector", 0, FIRST_SPLIT))]
        gpsimd_order = []
        done = 0
        for k in range(n_steps + 1):
            due = min(UNITS_BEFORE_STEP_0 + k, len(units))
            for i in range(done, due):
                if i + 1 < FIRST_UNITS:
                    vector_order.append((("weave vector", i + 1), loads_of(i + 1), weave, (i + 1, "vector", 0, FIRST_SPLIT)))
                shares = [("weave scalar", i)] + ([("weave gpsimd", i)] if i >= FIRST_UNITS else [])
                vector_order.append((("quantize",) + units[i], shares, quantize_unit, (i,)))
            done = due
            if k >= LAG:
                vector_order.append((("quantize y", k - LAG), [("round", k - LAG)], quantize_y, (k - LAG, 0, STEP)))
            if due + 1 < len(units):
                needs = loads_of(due + 1) + [("quantize",) + units[due - 1]]
                gpsimd_order.append((("weave gpsimd", due + 1), needs, weave, (due + 1, "gpsimd", LATER_SPLIT, UNIT)))
            if k >= 1:
                j, g = steps[k - 1]
                memory_load = ("m", g, chunk_of(MEMORY_BOUNDS, j * STEP))
                vector_order += [(("add", k - 1, u), [("turn", k - 1, u), memory_load], add_memory, (k - 1, u)) for u in range(2)]
            if k < n_steps:
                vector_order += [(("sum", k, u), [("clip a", k, u), ("product", k, u, 1)], clip_replica_b_and_add, (k, u))
                                 for u in range(2)]
        vector_order += [(("quantize y", h), [("round", h)], quantize_y, (h, 0, STEP)) for h in range(n_steps + 1 - LAG, last)]
        vector_order.append((("round", last, 1), [("round", last, 0)], round_y, (last, P, STEP, "vector")))
        vector_order.append((("quantize y", last, 0), [], quantize_y, (last, 0, P)))
        vector_order.append((("quantize y", last), [], quantize_y, (last, P, STEP)))

        tensor_order = []
        for h in range(n_steps + 1):
            if h < n_steps:
                j, g = steps[h]
                pairs = [(u, r) for r in range(2) for u in range(2)] if h == 0 else [(u, r) for u in range(2) for r in range(2)]
                for u, r in pairs:
                    needs = [("quantize", "z", r, j), ("quantize", "x", r, 0, g), ("quantize", "x", r, 1, g)]
                    tensor_order.append((("product", h, u, r), needs, product, (h, u, r)))
            if h >= 1:
                tensor_order += [(("turn", h - 1, u), [("sum", h - 1, u)], turn, (h - 1, u)) for u in range(2)]

        orders = [sync_order, scalar_order, vector_order, gpsimd_order, tensor_order]
        heads = [0] * len(orders)
        written = set()
        while any(heads[e] < len(order) for e, order in enumerate(orders)):
            before = sum(heads)
            for e, order in enumerate(orders):
                while heads[e] < len(order) and all(name in written for name in order[heads[e]][1]):
                    name, needs, call, args = order[heads[e]]
                    call(*args)
                    written.add(name)
                    heads[e] += 1
            assert sum(heads) > before
